import numpy as np
import ml_dtypes


def mxq(x, axis, fmt="e4m3"):
    dtype, down = {"e4m3": (ml_dtypes.float8_e4m3fn, 7), "e5m2": (ml_dtypes.float8_e5m2, 14)}[fmt]
    v = np.moveaxis(np.asarray(x, np.float32).astype(ml_dtypes.bfloat16).astype(np.float64), axis, -1)
    blocks = v.reshape(v.shape[:-1] + (-1, 32))
    amax = np.abs(blocks).max(-1, keepdims=True)
    byte = np.maximum(np.where(amax > 0, np.frexp(amax)[1] - 1 + 127, 0) - down, 1)
    scale = np.exp2(byte - 127.0)
    codes = (blocks / scale).astype(np.float32).astype(dtype).astype(np.float64)
    return np.moveaxis((codes * scale).reshape(v.shape), -1, axis)


WIDE = False


def mx_kscale(k):
    if not WIDE:
        return np.ones(k)
    levels = np.array([10, -10, 5, -5, 0])
    if k % 512:
        return np.exp2(np.random.permutation(np.resize(levels, k // 32))).repeat(32)
    a = np.empty((k // 512, 16))
    for p in range(k // 512):
        a[p, :8] = np.random.permutation(np.resize(levels, 8))
        for g in range(8):
            far = levels[np.abs(levels - a[p, g]) >= 10]
            a[p, g + 8] = far[np.random.randint(len(far))]
    return np.exp2(a.ravel()).repeat(32)


def f64(x):
    return np.asarray(x).astype(np.float64)


def striped(idx):
    return np.tile(idx.reshape(-1, 16).T, (8, 1)).astype(np.uint16)


def unstriped(offs):
    return offs[:16].T.reshape(-1).astype(np.int64)


E2M1 = np.array([0.0, 0.5, 1.0, 1.5, 2.0, 3.0, 4.0, 6.0, -0.0, -0.5, -1.0, -1.5, -2.0, -3.0, -4.0, -6.0])


def pack_weight(w, fmt):
    k, n = w.shape
    w = f64(np.asarray(w, np.float32).astype(ml_dtypes.bfloat16)).reshape(k // 32, 32, n)
    amax = np.abs(w).max(1)
    if fmt == "e4m3":
        byte = np.frexp(amax)[1] - 1 + 127 - 7
    else:
        mant, ex = np.frexp(amax / 6.0)
        byte = np.where(mant > 0.5, ex, ex - 1) + 127
    byte = np.clip(np.where(amax > 0, byte, 1), 1, 254)
    scaled = (w * np.exp2(127.0 - byte)[:, None, :]).reshape(k, n).astype(np.float32)
    by_word = np.ascontiguousarray(scaled.reshape(k // 512, 128, 4, n).transpose(0, 1, 3, 2))
    if fmt == "e4m3":
        words = by_word.astype(ml_dtypes.float8_e4m3fn).view(np.uint8)
    else:
        c = by_word.astype(ml_dtypes.float4_e2m1fn).view(np.uint8) & 0xF
        words = (c[..., 0::2] | (c[..., 1::2] << 4)).reshape(k // 512, 128, 2 * n)
    return np.ascontiguousarray(words), np.ascontiguousarray(byte.astype(np.uint8).reshape(k // 512, 16, n))


def unpack_weight(words, scales, fmt):
    g, _, n = scales.shape
    words = np.ascontiguousarray(words).reshape(g, 128, n, -1)
    if fmt == "e4m3":
        vals = words.view(ml_dtypes.float8_e4m3fn).astype(np.float64)
    else:
        nib = np.empty((g, 128, n, 4), np.uint8)
        nib[..., 0::2] = words & 0xF
        nib[..., 1::2] = words >> 4
        vals = E2M1[nib]
    vals = vals * np.repeat(np.exp2(scales.astype(np.float64) - 127.0), 8, axis=1)[..., None]
    return vals.transpose(0, 1, 3, 2).reshape(g * 512, n)


def gelu(v):
    return 0.5 * v * (1.0 + np.tanh(np.sqrt(2.0 / np.pi) * (v + 0.044715 * v**3)))


K, K2, H, N, T, S = 1024, 512, 1024, 384, 2048, 1024

def setup_inputs():
    n = np.random.standard_normal
    s = mx_kscale(K)[:, None]
    s2 = mx_kscale(K2)[:, None]
    u = mx_kscale(H)[:, None]
    d = {}
    d["tab_words"], d["tab_scales"] = pack_weight(n((K, T)) * s, "e4m3")
    d["offs"] = striped(np.random.permutation(T)[:S])
    d["xs_words"], d["xs_scales"] = pack_weight(n((K2, S)) * s2, "e4m3")
    d["w1"] = (n((K, H)) / s * u.T / K ** 0.5).astype(np.float32)
    d["c1"] = (0.5 * n(H) * u[:, 0]).astype(np.float32)
    d["w2_words"], d["w2_scales"] = pack_weight(n((K2, H)) / s2 * u.T / K2 ** 0.5, "e2m1")
    d["w3"] = (n((H, N)) / u / H ** 0.5).astype(np.float32)
    d["pol"] = np.exp(0.5 * n((N, S))).astype(np.float32)
    d["w4_words"], d["w4_scales"] = pack_weight(1.3 * n((H, N)) / u / H ** 0.5, "e4m3")
    d["c4"] = (0.6 * n(N)).astype(np.float32)
    d["w5_words"], d["w5_scales"] = pack_weight(0.7 * n((K, N)) / s / K ** 0.5, "e2m1")
    return d

def reference(tab_words, tab_scales, offs, xs_words, xs_scales, w1, c1, w2_words, w2_scales,
              w3, pol, w4_words, w4_scales, c4, w5_words, w5_scales):
    v = unpack_weight(tab_words, tab_scales, "e4m3")[:, unstriped(offs)]
    xs = unpack_weight(xs_words, xs_scales, "e4m3")
    w2 = unpack_weight(w2_words, w2_scales, "e2m1")
    w4 = unpack_weight(w4_words, w4_scales, "e4m3")
    w5 = unpack_weight(w5_words, w5_scales, "e2m1")
    offer = (mxq(f64(w1), 0, "e4m3").T @ v) + f64(c1)[:, None]
    need = w2.T @ xs
    hq = mxq(np.minimum(offer, need), 0, "e4m3")
    ruled = f64(pol) * (mxq(f64(w3), 0, "e4m3").T @ hq)
    plain = np.tanh((w4.T @ hq) + f64(c4)[:, None])
    own = w5.T @ v
    return ruled + plain + own

@@ -1,0 +1,275 @@
+from contextlib import ExitStack
+
+import concourse.mybir as mybir
+
+K, K2, H, N, T, S = 1024, 512, 1024, 384, 2048, 1024
+FLOPS = 2 * S * (K * H + K2 * H + 2 * H * N + K * N)
+
+F32 = mybir.dt.float32
+BF16 = mybir.dt.bfloat16
+I32 = mybir.dt.int32
+U32 = mybir.dt.uint32
+U16 = mybir.dt.uint16
+U8 = mybir.dt.uint8
+FP8X4 = mybir.dt.float8_e4m3fn_x4
+FP4X4 = mybir.dt.float4_e2m1fn_x4
+ALU = mybir.AluOpType
+ACT = mybir.ActivationFunctionType
+
+P = 128
+PASS = 512
+HALF = 512
+FINAL_ON_GPSIMD = True
+
+
+def tile_list_housing_shortlist_features_kernel(
+    tc, tab_words, tab_scales, offs, xs_words, xs_scales, w1, c1, w2_words, w2_scales,
+    w3, pol, w4_words, w4_scales, c4, w5_words, w5_scales, out,
+):
+    nc = tc.nc
+    with ExitStack() as ctx:
+        keep = ctx.enter_context(tc.tile_pool(name="keep", bufs=1))
+        ring3 = ctx.enter_context(tc.tile_pool(name="ring3", bufs=3))
+        psum = ctx.enter_context(tc.psum_pool(name="psum", bufs=1))
+
+        def held(name, shape, dtype, tag=None):
+            return keep.tile(shape, dtype, name=name, tag=tag or name, align_bytes=64)
+
+        banks = [psum.tile([P, 512], F32, name="bank%d" % b) for b in range(8)]
+        scalar_banks = banks[0:3]
+        vector_banks = banks[3:8]
+        turn = {"s": 0, "v": 0}
+
+        def next_bank(kind):
+            group = scalar_banks if kind == "s" else vector_banks
+            bank = group[turn[kind] % len(group)]
+            turn[kind] = turn[kind] + 1
+            return bank
+
+        offsets = held("offsets", [P, S // 16], U16)
+        tab_w = [held("tab_w%d" % a, [P, T], U32) for a in range(2)]
+        tab_s = held("tab_s", [P, T], U8)
+        xs_w = [held("xs_w%d" % h, [P, HALF], U32) for h in range(2)]
+        xs_s = held("xs_s", [P, S], U8)
+        w2_raw_w = held("w2_raw_w", [P, 2 * H], U8)
+        w2_raw_s = held("w2_raw_s", [P, H], U8)
+        w2_w = held("w2_w", [P, 2 * H], U8)
+        w2_s = held("w2_s", [P, H], U8)
+        w4_w = held("w4_w", [P, 2, N], U32)
+        w5_w = held("w5_w", [P, 2, 2 * N], U8)
+        c1_t = held("c1_t", [P, 2, 4], F32)
+        c4_t = held("c4_t", [P, 3], F32)
+        w1_raw = {(a, g): held("w1_raw%d%d" % (a, g), [P, 4, PASS], F32) for a in range(2) for g in range(2)}
+        w3_raw = [held("w3_raw%d" % a, [P, 4, N], F32) for a in range(2)]
+        pol_t = [held("pol%d" % h, [P, 3, HALF], F32) for h in range(2)]
+        v_w = {}
+        v_s = held("v_s", [P, S], U8)
+        v_s1 = held("v_s1", [P, S], U8)
+        w1_w = {}
+        w1_s = {(a, 0): w2_raw_s[4:P, a * PASS:(a + 1) * PASS] for a in range(2)}
+        for a in range(2):
+            w1_s[a, 1] = held("w1_s%d1" % a, [P, PASS], U8)[:]
+        w3_w = {}
+        late_s = held("late_s", [P, 2 * N], U8)
+        w3_b = held("w3_b", [P, 2 * N * 4], BF16)
+        h_w = {(g, h): held("h_w%d%d" % (g, h), [P, HALF], U32) for g in range(2) for h in range(2)}
+        h_s = {(g, h): held("h_s%d%d" % (g, h), [P, HALF], U8) for g in range(2) for h in range(2)}
+        warm_in = held("warm_in", [P, 8], F32)
+        warm_out = held("warm_out", [P, 8], F32)
+
+        for plane in (tab_s,):
+            nc.gpsimd.memset(plane[:].bitcast(I32), 0)
+        nc.vector.memset(xs_s[:].bitcast(I32), 0)
+        nc.vector.memset(warm_in[:], 0.0)
+        nc.vector.memset(v_s1[:].bitcast(I32), 0)
+
+        def load_w1(a, g):
+            rows = w1[a * PASS:(a + 1) * PASS, g * PASS:(g + 1) * PASS]
+            nc.sync.dma_start(out=w1_raw[a, g][:], in_=rows.rearrange("(p j) c -> p j c", j=4))
+
+        def load_tab(a):
+            nc.sync.dma_start(out=tab_w[a][:].bitcast(I32), in_=tab_words[a].rearrange("p t i -> p (t i)").bitcast(I32))
+
+        def load_xs(h):
+            words = xs_words[0].rearrange("p c i -> p (c i)").bitcast(I32)
+            nc.sync.dma_start(out=xs_w[h][:].bitcast(I32), in_=words[:, h * HALF:(h + 1) * HALF])
+
+        def load_plane(queue, first, scales):
+            for q in range(4):
+                rows = late_s[32 * q + first:32 * q + first + 4, :].rearrange("r (a c) -> r a c", a=2)
+                queue.dma_start(out=rows.bitcast(I32),
+                                in_=scales[:, 4 * q:4 * q + 4, :].rearrange("a r c -> r a c").bitcast(I32))
+
+        def load_plane1(queue, plane, scales):
+            for q in range(4):
+                queue.dma_start(out=plane[32 * q:32 * q + 4, :].bitcast(I32),
+                                in_=scales[0, 4 * q:4 * q + 4, :].bitcast(I32))
+
+        load_w1(0, 0)
+        nc.sync.dma_start(offsets[:], offs)
+        for q in range(4):
+            nc.scalar.dma_start(out=tab_s[32 * q:32 * q + 8, :].bitcast(I32),
+                                in_=tab_scales[:, 4 * q:4 * q + 4, :].bitcast(I32))
+        nc.scalar.activation(out=warm_out[:], in_=warm_in[:], func=ACT.Tanh)
+        load_plane1(nc.scalar, xs_s, xs_scales)
+        nc.sync.dma_start(out=w2_raw_w[:].bitcast(I32), in_=w2_words[0].bitcast(I32))
+        load_tab(0)
+        load_plane1(nc.sync, w2_raw_s, w2_scales)
+        load_w1(1, 0)
+        load_tab(1)
+        load_xs(0)
+        nc.sync.dma_start(out=c1_t[:], in_=c1.rearrange("(g p t) -> p g t", g=2, t=4))
+        load_w1(0, 1)
+        load_xs(1)
+        load_w1(1, 1)
+        nc.sync.dma_start(out=w5_w[:].bitcast(I32), in_=w5_words.rearrange("a p c -> p a c").bitcast(I32))
+        load_plane(nc.sync, 0, w5_scales)
+        for a in range(2):
+            nc.sync.dma_start(out=w3_raw[a][:], in_=w3[a * PASS:(a + 1) * PASS, :].rearrange("(p j) c -> p j c", j=4))
+            if a == 0:
+                load_plane(nc.sync, 8, w4_scales)
+        nc.sync.dma_start(out=w4_w[:].bitcast(I32), in_=w4_words.rearrange("a p c i -> p a (c i)").bitcast(I32))
+        with nc.allow_non_contiguous_dma(reason="one bias value to a partition"):
+            nc.sync.dma_start(out=c4_t[:], in_=c4.rearrange("(n p) -> p n", p=P))
+        for h in range(2):
+            nc.sync.dma_start(out=pol_t[h][:], in_=pol[:, h * HALF:(h + 1) * HALF].rearrange("(n p) j -> p n j", p=P))
+
+        def deal_w2_words():
+            nc.vector.tensor_copy(out=w2_w[:].rearrange("p (g t m b) -> p g m t b", g=2, t=4, b=2),
+                                  in_=w2_raw_w[:].rearrange("p (g m t b) -> p g m t b", g=2, t=4, b=2))
+
+        def deal_w2_scales(g):
+            gc = slice(g * PASS, (g + 1) * PASS)
+            nc.vector.tensor_copy(out=w2_s[:, gc].rearrange("p (t m) -> p m t", t=4),
+                                  in_=w2_raw_s[:, gc].rearrange("p (m t) -> p m t", t=4))
+
+        def listed(h):
+            return offsets[:, h * (HALF // 16):(h + 1) * (HALF // 16)]
+
+        def gather_words(a, h):
+            v_w[a, h] = held("v_w%d%d" % (a, h), [P, HALF], U32, tag="w1_b%d0" % h if a == 1 else None)
+            nc.vector.tensor_copy(out=v_w[a, h][:], in_=tab_w[a][:].indirect(listed(h)))
+
+        def gather_scales(h):
+            nc.vector.tensor_copy(out=v_s[:, h * HALF:(h + 1) * HALF], in_=tab_s[:].indirect(listed(h)))
+
+        w1_b = {}
+
+        def cast_w1(a, g):
+            tile = held("w1_b%d%d" % (a, g), [P, 4 * PASS], BF16)
+            w1_b[a, g] = tile
+            order = "p m j t" if g == 0 else "p m t j"
+            dst = tile[:].rearrange("p (t m j) -> " + order, t=4, j=4)
+            src = w1_raw[a, g][:].rearrange("p j (m t) -> " + order, t=4)
+            for m0 in range(0, P, 64):
+                if g == 0:
+                    nc.scalar.copy(out=dst[:, m0:m0 + 64], in_=src[:, m0:m0 + 64])
+                else:
+                    nc.gpsimd.tensor_scalar(out=dst[:, m0:m0 + 64], in0=src[:, m0:m0 + 64], scalar1=1.0, scalar2=0.0,
+                                            op0=ALU.mult, op1=ALU.add)
+
+        def quant_w1(a, g):
+            tag = None if g == 0 else ("offer00" if a == 0 else "h_b00")
+            w1_w[a, g] = held("w1_w%d%d" % (a, g), [P, PASS], U32, tag=tag)
+            nc.vector.quantize_mx(out=w1_w[a, g][:].bitcast(FP8X4), scales=w1_s[a, g], in_=w1_b[a, g][:])
+
+        def cast_w3(a):
+            dst = w3_b[:, a * 4 * N:(a + 1) * 4 * N].rearrange("p (c i j) -> p c j i", i=4, j=4)
+            src = w3_raw[a][:].rearrange("p j (c i) -> p c j i", i=4)
+            for c0 in range(0, N // 4, N // 8):
+                nc.gpsimd.tensor_scalar(out=dst[:, c0:c0 + N // 8], in0=src[:, c0:c0 + N // 8], scalar1=1.0, scalar2=0.0,
+                                        op0=ALU.mult, op1=ALU.add)
+
+        def quant_w3():
+            w3_w[0] = held("w3_w", [P, 2 * N], U32, tag="offer10")
+            for c0, c1_ in ((0, 512), (512, 768)):
+                nc.vector.quantize_mx(out=w3_w[0][:, c0:c1_].bitcast(FP8X4), scales=late_s[4:P, c0:c1_],
+                                      in_=w3_b[:, 4 * c0:4 * c1_])
+
+        def meet(g, h):
+            cols = slice(h * HALF, (h + 1) * HALF)
+            offer = held("offer%d%d" % (g, h), [P, 4, HALF], F32)
+            for t in range(4):
+                bank = next_bank("s")
+                wc = slice(t * P, (t + 1) * P)
+                for a in range(2):
+                    nc.tensor.matmul_mx(out=bank[:], lhsT=w1_w[a, g][:, wc].bitcast(FP8X4), lhsT_scale=w1_s[a, g][:, wc],
+                                        rhs=v_w[a, h][:].bitcast(FP8X4), rhs_scale=v_s[4 * a:P, cols],
+                                        start=(a == 0), stop=(a == 1))
+                nc.scalar.activation(out=offer[:, t, :], in_=bank[:], func=ACT.Identity, bias=c1_t[:, g, t:t + 1])
+            h_b = held("h_b%d%d" % (g, h), [P, 4 * HALF], BF16)
+            for q in range(4):
+                bank = next_bank("v")
+                for t in range(4):
+                    c0 = g * PASS + t * P
+                    nc.tensor.matmul_mx(out=bank[:, t * P:(t + 1) * P],
+                                        lhsT=w2_w[:, 2 * c0:2 * (c0 + P)].bitcast(FP4X4), lhsT_scale=w2_s[:, c0:c0 + P],
+                                        rhs=xs_w[h][:, q * P:(q + 1) * P].bitcast(FP8X4),
+                                        rhs_scale=xs_s[:, h * HALF + q * P:h * HALF + (q + 1) * P],
+                                        start=True, stop=True)
+                nc.vector.tensor_tensor(
+                    out=h_b[:, q * 4 * P:(q + 1) * 4 * P].rearrange("p (c i t) -> p c t i", i=4, t=4),
+                    in0=bank[:].rearrange("p (t c i) -> p c t i", t=4, i=4),
+                    in1=offer[:, :, q * P:(q + 1) * P].rearrange("p t (c i) -> p c t i", i=4),
+                    op=ALU.min)
+            nc.vector.quantize_mx(out=h_w[g, h][:].bitcast(FP8X4), scales=h_s[g, h][:], in_=h_b[:])
+
+        def read_out(h):
+            cols = slice(h * HALF, (h + 1) * HALF)
+            for n in range(3):
+                nc_ = slice(n * P, (n + 1) * P)
+                own = next_bank("v")
+                for a in range(2):
+                    plane = v_s if a == 0 else v_s1
+                    nc.tensor.matmul_mx(out=own[:], lhsT=w5_w[:, a, 2 * n * P:2 * (n + 1) * P].bitcast(FP4X4),
+                                        lhsT_scale=late_s[:, a * N + n * P:a * N + (n + 1) * P], rhs=v_w[a, h][:].bitcast(FP8X4),
+                                        rhs_scale=plane[:, cols], start=(a == 0), stop=(a == 1))
+                pre = next_bank("s")
+                for g in range(2):
+                    nc.tensor.matmul_mx(out=pre[:], lhsT=w4_w[:, g, nc_].bitcast(FP8X4), lhsT_scale=late_s[8:P, g * N + n * P:g * N + (n + 1) * P],
+                                        rhs=h_w[g, h][:].bitcast(FP8X4), rhs_scale=h_s[g, h][:],
+                                        start=(g == 0), stop=(g == 1))
+                raw = next_bank("v")
+                for g in range(2):
+                    wc = slice(g * N + n * P, g * N + (n + 1) * P)
+                    nc.tensor.matmul_mx(out=raw[:], lhsT=w3_w[0][:, wc].bitcast(FP8X4), lhsT_scale=late_s[4:P, wc],
+                                        rhs=h_w[g, h][:].bitcast(FP8X4), rhs_scale=h_s[g, h][:],
+                                        start=(g == 0), stop=(g == 1))
+                plain = ring3.tile([P, HALF], F32, name="plain")
+                nc.scalar.activation(out=plain[:], in_=pre[:], func=ACT.Tanh, bias=c4_t[:, n:n + 1])
+                part = ring3.tile([P, HALF], F32, name="part")
+                nc.vector.tensor_tensor(out=part[:], in0=own[:], in1=plain[:], op=ALU.add)
+                ruled = ring3.tile([P, HALF], F32, name="ruled")
+                nc.vector.tensor_tensor(out=ruled[:], in0=raw[:], in1=pol_t[h][:, n, :], op=ALU.mult)
+                total = ring3.tile([P, HALF], F32, name="total")
+                eng = nc.gpsimd if FINAL_ON_GPSIMD and (h, n) != (1, 2) else nc.vector
+                eng.tensor_tensor(out=total[:], in0=ruled[:], in1=part[:], op=ALU.add)
+                nc.sync.dma_start(out=out[nc_, cols], in_=total[:])
+
+        gather_scales(0)
+        gather_scales(1)
+        nc.gpsimd.dma_start(out=v_s1[0:100, :].bitcast(I32), in_=v_s[4:104, :].bitcast(I32))
+        cast_w1(0, 0)
+        gather_words(0, 0)
+        quant_w1(0, 0)
+        deal_w2_scales(0)
+        deal_w2_words()
+        gather_words(0, 1)
+        cast_w1(1, 0)
+        gather_words(1, 0)
+        quant_w1(1, 0)
+        deal_w2_scales(1)
+        gather_words(1, 1)
+        meet(0, 0)
+        cast_w1(0, 1)
+        quant_w1(0, 1)
+        cast_w1(1, 1)
+        meet(0, 1)
+        quant_w1(1, 1)
+        meet(1, 0)
+        cast_w3(0)
+        cast_w3(1)
+        quant_w3()
+        meet(1, 1)
+        read_out(0)
+        read_out(1)

@@ -29,7 +29,8 @@ def tile_list_housing_shortlist_features_kernel(
     nc = tc.nc
     with ExitStack() as ctx:
         keep = ctx.enter_context(tc.tile_pool(name="keep", bufs=1))
-        ring3 = ctx.enter_context(tc.tile_pool(name="ring3", bufs=3))
+        ring3 = ctx.enter_context(tc.tile_pool(name="ring3", bufs=6))
+        reuse = ctx.enter_context(tc.tile_pool(name="reuse", bufs=1))
         psum = ctx.enter_context(tc.psum_pool(name="psum", bufs=1))
 
         def held(name, shape, dtype, tag=None):
@@ -47,7 +48,7 @@ def tile_list_housing_shortlist_features_kernel(
             return bank
 
         offsets = held("offsets", [P, S // 16], U16)
-        tab_w = [held("tab_w%d" % a, [P, T], U32) for a in range(2)]
+        tab_w = [held("tab_w0", [P, T], U32), reuse.tile([P, T], U32, name="tab_w1", align_bytes=64, offset=0)]
         tab_s = held("tab_s", [P, T], U8)
         xs_w = [held("xs_w%d" % h, [P, HALF], U32) for h in range(2)]
         xs_s = held("xs_s", [P, S], U8)
@@ -63,6 +64,7 @@ def tile_list_housing_shortlist_features_kernel(
         w3_raw = [held("w3_raw%d" % a, [P, 4, N], F32) for a in range(2)]
         pol_t = [held("pol%d" % h, [P, 3, HALF], F32) for h in range(2)]
         v_w = {}
+        v_all = {}
         v_s = held("v_s", [P, S], U8)
         v_s1 = held("v_s1", [P, S], U8)
         w1_w = {}
@@ -71,7 +73,7 @@ def tile_list_housing_shortlist_features_kernel(
             w1_s[a, 1] = held("w1_s%d1" % a, [P, PASS], U8)[:]
         w3_w = {}
         late_s = held("late_s", [P, 2 * N], U8)
-        w3_b = held("w3_b", [P, 2 * N * 4], BF16)
+        w3_bs = {}
         h_w = {(g, h): held("h_w%d%d" % (g, h), [P, HALF], U32) for g in range(2) for h in range(2)}
         h_s = {(g, h): held("h_s%d%d" % (g, h), [P, HALF], U8) for g in range(2) for h in range(2)}
         warm_in = held("warm_in", [P, 8], F32)
@@ -79,7 +81,7 @@ def tile_list_housing_shortlist_features_kernel(
 
         for plane in (tab_s,):
             nc.gpsimd.memset(plane[:].bitcast(I32), 0)
-        nc.vector.memset(xs_s[:].bitcast(I32), 0)
+        nc.gpsimd.memset(xs_s[:].bitcast(I32), 0)
         nc.vector.memset(warm_in[:], 0.0)
         nc.vector.memset(v_s1[:].bitcast(I32), 0)
 
@@ -106,22 +108,22 @@ def tile_list_housing_shortlist_features_kernel(
                                 in_=scales[0, 4 * q:4 * q + 4, :].bitcast(I32))
 
         load_w1(0, 0)
+        load_tab(0)
         nc.sync.dma_start(offsets[:], offs)
         for q in range(4):
             nc.scalar.dma_start(out=tab_s[32 * q:32 * q + 8, :].bitcast(I32),
                                 in_=tab_scales[:, 4 * q:4 * q + 4, :].bitcast(I32))
         nc.scalar.activation(out=warm_out[:], in_=warm_in[:], func=ACT.Tanh)
-        load_plane1(nc.scalar, xs_s, xs_scales)
-        nc.sync.dma_start(out=w2_raw_w[:].bitcast(I32), in_=w2_words[0].bitcast(I32))
-        load_tab(0)
-        load_plane1(nc.sync, w2_raw_s, w2_scales)
+        load_plane1(nc.gpsimd, xs_s, xs_scales)
         load_w1(1, 0)
+        nc.sync.dma_start(out=w2_raw_w[:].bitcast(I32), in_=w2_words[0].bitcast(I32))
+        load_plane1(nc.sync, w2_raw_s, w2_scales)
+        load_w1(0, 1)
         load_tab(1)
         load_xs(0)
         nc.sync.dma_start(out=c1_t[:], in_=c1.rearrange("(g p t) -> p g t", g=2, t=4))
-        load_w1(0, 1)
-        load_xs(1)
         load_w1(1, 1)
+        load_xs(1)
         nc.sync.dma_start(out=w5_w[:].bitcast(I32), in_=w5_words.rearrange("a p c -> p a c").bitcast(I32))
         load_plane(nc.sync, 0, w5_scales)
         for a in range(2):
@@ -147,8 +149,10 @@ def tile_list_housing_shortlist_features_kernel(
             return offsets[:, h * (HALF // 16):(h + 1) * (HALF // 16)]
 
         def gather_words(a, h):
-            v_w[a, h] = held("v_w%d%d" % (a, h), [P, HALF], U32, tag="w1_b%d0" % h if a == 1 else None)
-            nc.vector.tensor_copy(out=v_w[a, h][:], in_=tab_w[a][:].indirect(listed(h)))
+            if h == 0:
+                v_all[a] = held("v_w%d" % a, [P, S], U32, tag="w1_b10" if a == 1 else None)
+            v_w[a, h] = v_all[a][:, h * HALF:(h + 1) * HALF]
+            nc.vector.tensor_copy(out=v_w[a, h], in_=tab_w[a][:].indirect(listed(h)))
 
         def gather_scales(h):
             nc.vector.tensor_copy(out=v_s[:, h * HALF:(h + 1) * HALF], in_=tab_s[:].indirect(listed(h)))
@@ -156,35 +160,41 @@ def tile_list_housing_shortlist_features_kernel(
         w1_b = {}
 
         def cast_w1(a, g):
-            tile = held("w1_b%d%d" % (a, g), [P, 4 * PASS], BF16)
+            if (a, g) == (1, 1):
+                tile = reuse.tile([P, 4 * PASS], BF16, name="w1_b11", align_bytes=64, offset=0)
+            else:
+                tile = held("w1_b%d%d" % (a, g), [P, 4 * PASS], BF16)
             w1_b[a, g] = tile
-            order = "p m j t" if g == 0 else "p m t j"
+            order = "p m j t"
             dst = tile[:].rearrange("p (t m j) -> " + order, t=4, j=4)
             src = w1_raw[a, g][:].rearrange("p j (m t) -> " + order, t=4)
             for m0 in range(0, P, 64):
-                if g == 0:
+                if (a, g) != (1, 1):
                     nc.scalar.copy(out=dst[:, m0:m0 + 64], in_=src[:, m0:m0 + 64])
-                else:
-                    nc.gpsimd.tensor_scalar(out=dst[:, m0:m0 + 64], in0=src[:, m0:m0 + 64], scalar1=1.0, scalar2=0.0,
-                                            op0=ALU.mult, op1=ALU.add)
+            if (a, g) == (1, 1):
+                nc.vector.tensor_copy(out=dst, in_=src)
 
         def quant_w1(a, g):
-            tag = None if g == 0 else ("offer00" if a == 0 else "h_b00")
-            w1_w[a, g] = held("w1_w%d%d" % (a, g), [P, PASS], U32, tag=tag)
+            if (a, g) == (0, 1):
+                w1_w[a, g] = reuse.tile([P, PASS], U32, name="w1_w01", align_bytes=64, offset=4096)
+            else:
+                w1_w[a, g] = held("w1_w%d%d" % (a, g), [P, PASS], U32)
             nc.vector.quantize_mx(out=w1_w[a, g][:].bitcast(FP8X4), scales=w1_s[a, g], in_=w1_b[a, g][:])
 
         def cast_w3(a):
+            if a == 0:
+                w3_bs[0] = held("w3_b", [P, 2 * N * 4], BF16, tag="offer00")
+            w3_b = w3_bs[0]
             dst = w3_b[:, a * 4 * N:(a + 1) * 4 * N].rearrange("p (c i j) -> p c j i", i=4, j=4)
             src = w3_raw[a][:].rearrange("p j (c i) -> p c j i", i=4)
             for c0 in range(0, N // 4, N // 8):
-                nc.gpsimd.tensor_scalar(out=dst[:, c0:c0 + N // 8], in0=src[:, c0:c0 + N // 8], scalar1=1.0, scalar2=0.0,
-                                        op0=ALU.mult, op1=ALU.add)
+                nc.scalar.copy(out=dst[:, c0:c0 + N // 8], in_=src[:, c0:c0 + N // 8])
 
         def quant_w3():
             w3_w[0] = held("w3_w", [P, 2 * N], U32, tag="offer10")
             for c0, c1_ in ((0, 512), (512, 768)):
                 nc.vector.quantize_mx(out=w3_w[0][:, c0:c1_].bitcast(FP8X4), scales=late_s[4:P, c0:c1_],
-                                      in_=w3_b[:, 4 * c0:4 * c1_])
+                                      in_=w3_bs[0][:, 4 * c0:4 * c1_])
 
         def meet(g, h):
             cols = slice(h * HALF, (h + 1) * HALF)
@@ -194,7 +204,7 @@ def tile_list_housing_shortlist_features_kernel(
                 wc = slice(t * P, (t + 1) * P)
                 for a in range(2):
                     nc.tensor.matmul_mx(out=bank[:], lhsT=w1_w[a, g][:, wc].bitcast(FP8X4), lhsT_scale=w1_s[a, g][:, wc],
-                                        rhs=v_w[a, h][:].bitcast(FP8X4), rhs_scale=v_s[4 * a:P, cols],
+                                        rhs=v_w[a, h].bitcast(FP8X4), rhs_scale=v_s[4 * a:P, cols],
                                         start=(a == 0), stop=(a == 1))
                 nc.scalar.activation(out=offer[:, t, :], in_=bank[:], func=ACT.Identity, bias=c1_t[:, g, t:t + 1])
             h_b = held("h_b%d%d" % (g, h), [P, 4 * HALF], BF16)
@@ -216,29 +226,34 @@ def tile_list_housing_shortlist_features_kernel(
 
         def read_out(h):
             cols = slice(h * HALF, (h + 1) * HALF)
+            plain = {}
+            for n in range(3):
+                nc_ = slice(n * P, (n + 1) * P)
+                pre = next_bank("s")
+                for g in range(2):
+                    nc.tensor.matmul_mx(out=pre[:], lhsT=w4_w[:, g, nc_].bitcast(FP8X4),
+                                        lhsT_scale=late_s[8:P, g * N + n * P:g * N + (n + 1) * P],
+                                        rhs=h_w[g, h][:].bitcast(FP8X4), rhs_scale=h_s[g, h][:],
+                                        start=(g == 0), stop=(g == 1))
+                plain[n] = ring3.tile([P, HALF], F32, name="plain")
+                nc.scalar.activation(out=plain[n][:], in_=pre[:], func=ACT.Tanh, bias=c4_t[:, n:n + 1])
             for n in range(3):
                 nc_ = slice(n * P, (n + 1) * P)
                 own = next_bank("v")
                 for a in range(2):
                     plane = v_s if a == 0 else v_s1
                     nc.tensor.matmul_mx(out=own[:], lhsT=w5_w[:, a, 2 * n * P:2 * (n + 1) * P].bitcast(FP4X4),
-                                        lhsT_scale=late_s[:, a * N + n * P:a * N + (n + 1) * P], rhs=v_w[a, h][:].bitcast(FP8X4),
+                                        lhsT_scale=late_s[:, a * N + n * P:a * N + (n + 1) * P],
+                                        rhs=v_w[a, h].bitcast(FP8X4),
                                         rhs_scale=plane[:, cols], start=(a == 0), stop=(a == 1))
-                pre = next_bank("s")
-                for g in range(2):
-                    nc.tensor.matmul_mx(out=pre[:], lhsT=w4_w[:, g, nc_].bitcast(FP8X4), lhsT_scale=late_s[8:P, g * N + n * P:g * N + (n + 1) * P],
-                                        rhs=h_w[g, h][:].bitcast(FP8X4), rhs_scale=h_s[g, h][:],
-                                        start=(g == 0), stop=(g == 1))
                 raw = next_bank("v")
                 for g in range(2):
                     wc = slice(g * N + n * P, g * N + (n + 1) * P)
                     nc.tensor.matmul_mx(out=raw[:], lhsT=w3_w[0][:, wc].bitcast(FP8X4), lhsT_scale=late_s[4:P, wc],
                                         rhs=h_w[g, h][:].bitcast(FP8X4), rhs_scale=h_s[g, h][:],
                                         start=(g == 0), stop=(g == 1))
-                plain = ring3.tile([P, HALF], F32, name="plain")
-                nc.scalar.activation(out=plain[:], in_=pre[:], func=ACT.Tanh, bias=c4_t[:, n:n + 1])
                 part = ring3.tile([P, HALF], F32, name="part")
-                nc.vector.tensor_tensor(out=part[:], in0=own[:], in1=plain[:], op=ALU.add)
+                nc.vector.tensor_tensor(out=part[:], in0=own[:], in1=plain[n][:], op=ALU.add)
                 ruled = ring3.tile([P, HALF], F32, name="ruled")
                 nc.vector.tensor_tensor(out=ruled[:], in0=raw[:], in1=pol_t[h][:, n, :], op=ALU.mult)
                 total = ring3.tile([P, HALF], F32, name="total")
@@ -251,21 +266,21 @@ def tile_list_housing_shortlist_features_kernel(
         nc.gpsimd.dma_start(out=v_s1[0:100, :].bitcast(I32), in_=v_s[4:104, :].bitcast(I32))
         cast_w1(0, 0)
         gather_words(0, 0)
+        gather_words(0, 1)
         quant_w1(0, 0)
         deal_w2_scales(0)
         deal_w2_words()
-        gather_words(0, 1)
         cast_w1(1, 0)
-        gather_words(1, 0)
         quant_w1(1, 0)
         deal_w2_scales(1)
-        gather_words(1, 1)
-        meet(0, 0)
         cast_w1(0, 1)
+        gather_words(1, 0)
+        gather_words(1, 1)
         quant_w1(0, 1)
         cast_w1(1, 1)
-        meet(0, 1)
         quant_w1(1, 1)
+        meet(0, 0)
+        meet(0, 1)
         meet(1, 0)
         cast_w3(0)
         cast_w3(1)

@@ -79,9 +79,8 @@ def tile_list_housing_shortlist_features_kernel(
         warm_in = held("warm_in", [P, 8], F32)
         warm_out = held("warm_out", [P, 8], F32)
 
-        for plane in (tab_s,):
-            nc.gpsimd.memset(plane[:].bitcast(I32), 0)
-        nc.gpsimd.memset(xs_s[:].bitcast(I32), 0)
+        nc.gpsimd.memset(tab_s[:].bitcast(I32), 0)
+        nc.vector.memset(xs_s[:].bitcast(I32), 0)
         nc.vector.memset(warm_in[:], 0.0)
         nc.vector.memset(v_s1[:].bitcast(I32), 0)
 
@@ -107,32 +106,32 @@ def tile_list_housing_shortlist_features_kernel(
                 queue.dma_start(out=plane[32 * q:32 * q + 4, :].bitcast(I32),
                                 in_=scales[0, 4 * q:4 * q + 4, :].bitcast(I32))
 
+        nc.sync.dma_start(offsets[:], offs)
         load_w1(0, 0)
         load_tab(0)
-        nc.sync.dma_start(offsets[:], offs)
         for q in range(4):
-            nc.scalar.dma_start(out=tab_s[32 * q:32 * q + 8, :].bitcast(I32),
+            nc.gpsimd.dma_start(out=tab_s[32 * q:32 * q + 8, :].bitcast(I32),
                                 in_=tab_scales[:, 4 * q:4 * q + 4, :].bitcast(I32))
         nc.scalar.activation(out=warm_out[:], in_=warm_in[:], func=ACT.Tanh)
+        load_plane1(nc.gpsimd, w2_raw_s, w2_scales)
         load_plane1(nc.gpsimd, xs_s, xs_scales)
         load_w1(1, 0)
         nc.sync.dma_start(out=w2_raw_w[:].bitcast(I32), in_=w2_words[0].bitcast(I32))
-        load_plane1(nc.sync, w2_raw_s, w2_scales)
         load_w1(0, 1)
         load_tab(1)
         load_xs(0)
-        nc.sync.dma_start(out=c1_t[:], in_=c1.rearrange("(g p t) -> p g t", g=2, t=4))
+        nc.gpsimd.dma_start(out=c1_t[:], in_=c1.rearrange("(g p t) -> p g t", g=2, t=4))
         load_w1(1, 1)
         load_xs(1)
         nc.sync.dma_start(out=w5_w[:].bitcast(I32), in_=w5_words.rearrange("a p c -> p a c").bitcast(I32))
-        load_plane(nc.sync, 0, w5_scales)
+        load_plane(nc.gpsimd, 0, w5_scales)
         for a in range(2):
             nc.sync.dma_start(out=w3_raw[a][:], in_=w3[a * PASS:(a + 1) * PASS, :].rearrange("(p j) c -> p j c", j=4))
             if a == 0:
-                load_plane(nc.sync, 8, w4_scales)
+                load_plane(nc.gpsimd, 8, w4_scales)
         nc.sync.dma_start(out=w4_w[:].bitcast(I32), in_=w4_words.rearrange("a p c i -> p a (c i)").bitcast(I32))
         with nc.allow_non_contiguous_dma(reason="one bias value to a partition"):
-            nc.sync.dma_start(out=c4_t[:], in_=c4.rearrange("(n p) -> p n", p=P))
+            nc.gpsimd.dma_start(out=c4_t[:], in_=c4.rearrange("(n p) -> p n", p=P))
         for h in range(2):
             nc.sync.dma_start(out=pol_t[h][:], in_=pol[:, h * HALF:(h + 1) * HALF].rearrange("(n p) j -> p n j", p=P))
 
@@ -246,20 +245,25 @@ def tile_list_housing_shortlist_features_kernel(
                                         lhsT_scale=late_s[:, a * N + n * P:a * N + (n + 1) * P],
                                         rhs=v_w[a, h].bitcast(FP8X4),
                                         rhs_scale=plane[:, cols], start=(a == 0), stop=(a == 1))
-                raw = next_bank("v")
-                for g in range(2):
-                    wc = slice(g * N + n * P, g * N + (n + 1) * P)
-                    nc.tensor.matmul_mx(out=raw[:], lhsT=w3_w[0][:, wc].bitcast(FP8X4), lhsT_scale=late_s[4:P, wc],
-                                        rhs=h_w[g, h][:].bitcast(FP8X4), rhs_scale=h_s[g, h][:],
-                                        start=(g == 0), stop=(g == 1))
                 part = ring3.tile([P, HALF], F32, name="part")
                 nc.vector.tensor_tensor(out=part[:], in0=own[:], in1=plain[n][:], op=ALU.add)
-                ruled = ring3.tile([P, HALF], F32, name="ruled")
-                nc.vector.tensor_tensor(out=ruled[:], in0=raw[:], in1=pol_t[h][:, n, :], op=ALU.mult)
-                total = ring3.tile([P, HALF], F32, name="total")
-                eng = nc.gpsimd if FINAL_ON_GPSIMD and (h, n) != (1, 2) else nc.vector
-                eng.tensor_tensor(out=total[:], in0=ruled[:], in1=part[:], op=ALU.add)
-                nc.sync.dma_start(out=out[nc_, cols], in_=total[:])
+                last = (h, n) == (1, 2)
+                width = HALF // 2 if last else HALF
+                for c0 in range(0, HALF, width):
+                    pc = slice(c0, c0 + width)
+                    raw = next_bank("v")
+                    for g in range(2):
+                        wc = slice(g * N + n * P, g * N + (n + 1) * P)
+                        nc.tensor.matmul_mx(out=raw[:, 0:width], lhsT=w3_w[0][:, wc].bitcast(FP8X4),
+                                            lhsT_scale=late_s[4:P, wc],
+                                            rhs=h_w[g, h][:, pc].bitcast(FP8X4), rhs_scale=h_s[g, h][:, pc],
+                                            start=(g == 0), stop=(g == 1))
+                    ruled = ring3.tile([P, width], F32, name="ruled")
+                    nc.vector.tensor_tensor(out=ruled[:], in0=raw[:, 0:width], in1=pol_t[h][:, n, pc], op=ALU.mult)
+                    total = ring3.tile([P, width], F32, name="total")
+                    eng = nc.gpsimd if FINAL_ON_GPSIMD and not last else nc.vector
+                    eng.tensor_tensor(out=total[:], in0=ruled[:], in1=part[:, pc], op=ALU.add)
+                    nc.sync.dma_start(out=out[nc_, h * HALF + c0:h * HALF + c0 + width], in_=total[:])
 
         gather_scales(0)
         gather_scales(1)

@@ -68,19 +68,20 @@ def tile_list_housing_shortlist_features_kernel(
         v_s = held("v_s", [P, S], U8)
         v_s1 = held("v_s1", [P, S], U8)
         w1_w = {}
-        w1_s = {(a, 0): w2_raw_s[4:P, a * PASS:(a + 1) * PASS] for a in range(2)}
-        for a in range(2):
-            w1_s[a, 1] = held("w1_s%d1" % a, [P, PASS], U8)[:]
+        w1_s = {(0, 0): w2_raw_s[4:P, 0:PASS], (1, 0): xs_s[4:P, 0:PASS],
+                (0, 1): xs_s[4:P, PASS:2 * PASS], (1, 1): w2_raw_s[4:P, PASS:2 * PASS]}
         w3_w = {}
-        late_s = held("late_s", [P, 2 * N], U8)
+        late_s = held("late_s", [P, S], U8)
+        w3_s = held("w3_s", [P, 2 * N], U8)
         w3_bs = {}
         h_w = {(g, h): held("h_w%d%d" % (g, h), [P, HALF], U32) for g in range(2) for h in range(2)}
-        h_s = {(g, h): held("h_s%d%d" % (g, h), [P, HALF], U8) for g in range(2) for h in range(2)}
+        h_s = {(0, h): late_s[4:P, h * HALF:(h + 1) * HALF] for h in range(2)}
+        for h in range(2):
+            h_s[1, h] = held("h_s1%d" % h, [P, HALF], U8)[:]
         warm_in = held("warm_in", [P, 8], F32)
         warm_out = held("warm_out", [P, 8], F32)
 
         nc.gpsimd.memset(tab_s[:].bitcast(I32), 0)
-        nc.vector.memset(xs_s[:].bitcast(I32), 0)
         nc.vector.memset(warm_in[:], 0.0)
         nc.vector.memset(v_s1[:].bitcast(I32), 0)
 
@@ -97,7 +98,7 @@ def tile_list_housing_shortlist_features_kernel(
 
         def load_plane(queue, first, scales):
             for q in range(4):
-                rows = late_s[32 * q + first:32 * q + first + 4, :].rearrange("r (a c) -> r a c", a=2)
+                rows = late_s[32 * q + first:32 * q + first + 4, 0:2 * N].rearrange("r (a c) -> r a c", a=2)
                 queue.dma_start(out=rows.bitcast(I32),
                                 in_=scales[:, 4 * q:4 * q + 4, :].rearrange("a r c -> r a c").bitcast(I32))
 
@@ -108,36 +109,35 @@ def tile_list_housing_shortlist_features_kernel(
 
         nc.sync.dma_start(offsets[:], offs)
         load_w1(0, 0)
-        load_tab(0)
+        nc.sync.dma_start(out=w2_raw_w[:].bitcast(I32), in_=w2_words[0].bitcast(I32))
+        nc.sync.dma_start(out=c1_t[:], in_=c1.rearrange("(g p t) -> p g t", g=2, t=4))
         for q in range(4):
-            nc.gpsimd.dma_start(out=tab_s[32 * q:32 * q + 8, :].bitcast(I32),
+            nc.scalar.dma_start(out=tab_s[32 * q:32 * q + 8, :].bitcast(I32),
                                 in_=tab_scales[:, 4 * q:4 * q + 4, :].bitcast(I32))
         nc.scalar.activation(out=warm_out[:], in_=warm_in[:], func=ACT.Tanh)
-        load_plane1(nc.gpsimd, w2_raw_s, w2_scales)
-        load_plane1(nc.gpsimd, xs_s, xs_scales)
+        load_tab(0)
         load_w1(1, 0)
-        nc.sync.dma_start(out=w2_raw_w[:].bitcast(I32), in_=w2_words[0].bitcast(I32))
-        load_w1(0, 1)
+        load_plane1(nc.sync, w2_raw_s, w2_scales)
         load_tab(1)
+        load_plane1(nc.sync, xs_s, xs_scales)
+        load_w1(0, 1)
         load_xs(0)
-        nc.gpsimd.dma_start(out=c1_t[:], in_=c1.rearrange("(g p t) -> p g t", g=2, t=4))
+        load_plane(nc.sync, 0, w5_scales)
         load_w1(1, 1)
         load_xs(1)
-        nc.sync.dma_start(out=w5_w[:].bitcast(I32), in_=w5_words.rearrange("a p c -> p a c").bitcast(I32))
-        load_plane(nc.gpsimd, 0, w5_scales)
+        load_plane(nc.sync, 8, w4_scales)
         for a in range(2):
             nc.sync.dma_start(out=w3_raw[a][:], in_=w3[a * PASS:(a + 1) * PASS, :].rearrange("(p j) c -> p j c", j=4))
-            if a == 0:
-                load_plane(nc.gpsimd, 8, w4_scales)
+        nc.sync.dma_start(out=w5_w[:].bitcast(I32), in_=w5_words.rearrange("a p c -> p a c").bitcast(I32))
         nc.sync.dma_start(out=w4_w[:].bitcast(I32), in_=w4_words.rearrange("a p c i -> p a (c i)").bitcast(I32))
         with nc.allow_non_contiguous_dma(reason="one bias value to a partition"):
-            nc.gpsimd.dma_start(out=c4_t[:], in_=c4.rearrange("(n p) -> p n", p=P))
+            nc.sync.dma_start(out=c4_t[:], in_=c4.rearrange("(n p) -> p n", p=P))
         for h in range(2):
             nc.sync.dma_start(out=pol_t[h][:], in_=pol[:, h * HALF:(h + 1) * HALF].rearrange("(n p) j -> p n j", p=P))
 
         def deal_w2_words():
-            nc.vector.tensor_copy(out=w2_w[:].rearrange("p (g t m b) -> p g m t b", g=2, t=4, b=2),
-                                  in_=w2_raw_w[:].rearrange("p (g m t b) -> p g m t b", g=2, t=4, b=2))
+            nc.vector.tensor_copy(out=w2_w[:].bitcast(U16).rearrange("p (g t m) -> p g m t", g=2, t=4),
+                                  in_=w2_raw_w[:].bitcast(U16).rearrange("p (g m t) -> p g m t", g=2, t=4))
 
         def deal_w2_scales(g):
             gc = slice(g * PASS, (g + 1) * PASS)
@@ -159,45 +159,58 @@ def tile_list_housing_shortlist_features_kernel(
         w1_b = {}
 
         def cast_w1(a, g):
-            if (a, g) == (1, 1):
-                tile = reuse.tile([P, 4 * PASS], BF16, name="w1_b11", align_bytes=64, offset=0)
+            if (a, g) == (0, 1):
+                tile = reuse.tile([P, 4 * PASS], BF16, name="w1_b01", align_bytes=64, offset=0)
             else:
                 tile = held("w1_b%d%d" % (a, g), [P, 4 * PASS], BF16)
             w1_b[a, g] = tile
-            order = "p m j t"
+            order = "p m t j" if (a, g) == (1, 1) else "p m j t"
             dst = tile[:].rearrange("p (t m j) -> " + order, t=4, j=4)
             src = w1_raw[a, g][:].rearrange("p j (m t) -> " + order, t=4)
             for m0 in range(0, P, 64):
-                if (a, g) != (1, 1):
+                if g == 0:
                     nc.scalar.copy(out=dst[:, m0:m0 + 64], in_=src[:, m0:m0 + 64])
-            if (a, g) == (1, 1):
+                elif a == 1:
+                    nc.gpsimd.tensor_scalar(out=dst[:, m0:m0 + 64], in0=src[:, m0:m0 + 64], scalar1=1.0, scalar2=0.0,
+                                            op0=ALU.mult, op1=ALU.add)
+            if (a, g) == (0, 1):
                 nc.vector.tensor_copy(out=dst, in_=src)
 
         def quant_w1(a, g):
-            if (a, g) == (0, 1):
-                w1_w[a, g] = reuse.tile([P, PASS], U32, name="w1_w01", align_bytes=64, offset=4096)
+            if (a, g) == (1, 1):
+                w1_w[a, g] = reuse.tile([P, PASS], U32, name="w1_w11", align_bytes=64, offset=8192)
             else:
                 w1_w[a, g] = held("w1_w%d%d" % (a, g), [P, PASS], U32)
             nc.vector.quantize_mx(out=w1_w[a, g][:].bitcast(FP8X4), scales=w1_s[a, g], in_=w1_b[a, g][:])
 
         def cast_w3(a):
             if a == 0:
-                w3_bs[0] = held("w3_b", [P, 2 * N * 4], BF16, tag="offer00")
-            w3_b = w3_bs[0]
-            dst = w3_b[:, a * 4 * N:(a + 1) * 4 * N].rearrange("p (c i j) -> p c j i", i=4, j=4)
+                w3_bs[a] = reuse.tile([P, N * 4], BF16, name="w3_b0", align_bytes=64, offset=8192 + 2048)
+            else:
+                w3_bs[a] = held("w3_b1", [P, N * 4], BF16, tag="offer01")
+            dst = w3_bs[a][:].rearrange("p (c i j) -> p c j i", i=4, j=4)
             src = w3_raw[a][:].rearrange("p j (c i) -> p c j i", i=4)
             for c0 in range(0, N // 4, N // 8):
                 nc.scalar.copy(out=dst[:, c0:c0 + N // 8], in_=src[:, c0:c0 + N // 8])
 
-        def quant_w3():
-            w3_w[0] = held("w3_w", [P, 2 * N], U32, tag="offer10")
-            for c0, c1_ in ((0, 512), (512, 768)):
-                nc.vector.quantize_mx(out=w3_w[0][:, c0:c1_].bitcast(FP8X4), scales=late_s[4:P, c0:c1_],
-                                      in_=w3_bs[0][:, 4 * c0:4 * c1_])
+        def quant_w3(a):
+            if a == 0:
+                w3_w[0] = held("w3_w", [P, 2 * N], U32)
+            for c0, c1_ in ((0, 256), (256, 384)):
+                nc.vector.quantize_mx(out=w3_w[0][:, a * N + c0:a * N + c1_].bitcast(FP8X4),
+                                      scales=w3_s[:, a * N + c0:a * N + c1_], in_=w3_bs[a][:, 4 * c0:4 * c1_])
 
-        def meet(g, h):
+        h_bs = {}
+
+        def quant_h(g, h):
+            nc.vector.quantize_mx(out=h_w[g, h][:].bitcast(FP8X4), scales=h_s[g, h], in_=h_bs[g, h][:])
+
+        def meet(g, h, after_first=None):
             cols = slice(h * HALF, (h + 1) * HALF)
-            offer = held("offer%d%d" % (g, h), [P, 4, HALF], F32)
+            if (g, h) == (0, 0):
+                offer = reuse.tile([P, 4, HALF], F32, name="offer00", align_bytes=64, offset=8192)
+            else:
+                offer = held("offer%d%d" % (g, h), [P, 4, HALF], F32)
             for t in range(4):
                 bank = next_bank("s")
                 wc = slice(t * P, (t + 1) * P)
@@ -207,6 +220,7 @@ def tile_list_housing_shortlist_features_kernel(
                                         start=(a == 0), stop=(a == 1))
                 nc.scalar.activation(out=offer[:, t, :], in_=bank[:], func=ACT.Identity, bias=c1_t[:, g, t:t + 1])
             h_b = held("h_b%d%d" % (g, h), [P, 4 * HALF], BF16)
+            h_bs[g, h] = h_b
             for q in range(4):
                 bank = next_bank("v")
                 for t in range(4):
@@ -221,9 +235,10 @@ def tile_list_housing_shortlist_features_kernel(
                     in0=bank[:].rearrange("p (t c i) -> p c t i", t=4, i=4),
                     in1=offer[:, :, q * P:(q + 1) * P].rearrange("p t (c i) -> p c t i", i=4),
                     op=ALU.min)
-            nc.vector.quantize_mx(out=h_w[g, h][:].bitcast(FP8X4), scales=h_s[g, h][:], in_=h_b[:])
+                if q == 0 and after_first is not None:
+                    after_first()
 
-        def read_out(h):
+        def read_out(h, after_first=None):
             cols = slice(h * HALF, (h + 1) * HALF)
             plain = {}
             for n in range(3):
@@ -232,7 +247,7 @@ def tile_list_housing_shortlist_features_kernel(
                 for g in range(2):
                     nc.tensor.matmul_mx(out=pre[:], lhsT=w4_w[:, g, nc_].bitcast(FP8X4),
                                         lhsT_scale=late_s[8:P, g * N + n * P:g * N + (n + 1) * P],
-                                        rhs=h_w[g, h][:].bitcast(FP8X4), rhs_scale=h_s[g, h][:],
+                                        rhs=h_w[g, h][:].bitcast(FP8X4), rhs_scale=h_s[g, h],
                                         start=(g == 0), stop=(g == 1))
                 plain[n] = ring3.tile([P, HALF], F32, name="plain")
                 nc.scalar.activation(out=plain[n][:], in_=pre[:], func=ACT.Tanh, bias=c4_t[:, n:n + 1])
@@ -247,6 +262,8 @@ def tile_list_housing_shortlist_features_kernel(
                                         rhs_scale=plane[:, cols], start=(a == 0), stop=(a == 1))
                 part = ring3.tile([P, HALF], F32, name="part")
                 nc.vector.tensor_tensor(out=part[:], in0=own[:], in1=plain[n][:], op=ALU.add)
+                if n == 0 and after_first is not None:
+                    after_first()
                 last = (h, n) == (1, 2)
                 width = HALF // 2 if last else HALF
                 for c0 in range(0, HALF, width):
@@ -255,7 +272,7 @@ def tile_list_housing_shortlist_features_kernel(
                     for g in range(2):
                         wc = slice(g * N + n * P, g * N + (n + 1) * P)
                         nc.tensor.matmul_mx(out=raw[:, 0:width], lhsT=w3_w[0][:, wc].bitcast(FP8X4),
-                                            lhsT_scale=late_s[4:P, wc],
+                                            lhsT_scale=w3_s[:, wc],
                                             rhs=h_w[g, h][:, pc].bitcast(FP8X4), rhs_scale=h_s[g, h][:, pc],
                                             start=(g == 0), stop=(g == 1))
                     ruled = ring3.tile([P, width], F32, name="ruled")
@@ -265,6 +282,7 @@ def tile_list_housing_shortlist_features_kernel(
                     eng.tensor_tensor(out=total[:], in0=ruled[:], in1=part[:, pc], op=ALU.add)
                     nc.sync.dma_start(out=out[nc_, h * HALF + c0:h * HALF + c0 + width], in_=total[:])
 
+        deal_w2_words()
         gather_scales(0)
         gather_scales(1)
         nc.gpsimd.dma_start(out=v_s1[0:100, :].bitcast(I32), in_=v_s[4:104, :].bitcast(I32))
@@ -273,22 +291,22 @@ def tile_list_housing_shortlist_features_kernel(
         gather_words(0, 1)
         quant_w1(0, 0)
         deal_w2_scales(0)
-        deal_w2_words()
         cast_w1(1, 0)
         quant_w1(1, 0)
-        deal_w2_scales(1)
-        cast_w1(0, 1)
         gather_words(1, 0)
         gather_words(1, 1)
+        cast_w1(0, 1)
         quant_w1(0, 1)
         cast_w1(1, 1)
-        quant_w1(1, 1)
         meet(0, 0)
-        meet(0, 1)
-        meet(1, 0)
+        quant_w1(1, 1)
+        deal_w2_scales(1)
+        meet(0, 1, lambda: quant_h(0, 0))
         cast_w3(0)
+        meet(1, 0, lambda: quant_h(0, 1))
         cast_w3(1)
-        quant_w3()
-        meet(1, 1)
-        read_out(0)
+        quant_w3(0)
+        quant_w3(1)
+        meet(1, 1, lambda: quant_h(1, 0))
+        read_out(0, lambda: quant_h(1, 1))
         read_out(1)

@@ -17,9 +17,15 @@ ALU = mybir.AluOpType
 ACT = mybir.ActivationFunctionType
 
 P = 128
-PASS = 512
+PACK = 4
+PASS = P * PACK
 HALF = 512
-FINAL_ON_GPSIMD = True
+QUADRANTS = 4
+N_TILES = N // P
+PER_COLUMN = 16
+SCALAR_BANKS = 3
+STAGE_BUFS = 2 * N_TILES
+LIVE_ROWS = 100
 
 
 def tile_list_housing_shortlist_features_kernel(
@@ -29,284 +35,283 @@ def tile_list_housing_shortlist_features_kernel(
     nc = tc.nc
     with ExitStack() as ctx:
         keep = ctx.enter_context(tc.tile_pool(name="keep", bufs=1))
-        ring3 = ctx.enter_context(tc.tile_pool(name="ring3", bufs=6))
+        stage = ctx.enter_context(tc.tile_pool(name="stage", bufs=STAGE_BUFS))
         reuse = ctx.enter_context(tc.tile_pool(name="reuse", bufs=1))
         psum = ctx.enter_context(tc.psum_pool(name="psum", bufs=1))
 
         def held(name, shape, dtype, tag=None):
             return keep.tile(shape, dtype, name=name, tag=tag or name, align_bytes=64)
 
-        banks = [psum.tile([P, 512], F32, name="bank%d" % b) for b in range(8)]
-        scalar_banks = banks[0:3]
-        vector_banks = banks[3:8]
-        turn = {"s": 0, "v": 0}
+        def placed(name, shape, dtype, offset):
+            return reuse.tile(shape, dtype, name=name, align_bytes=64, offset=offset)
 
-        def next_bank(kind):
-            group = scalar_banks if kind == "s" else vector_banks
-            bank = group[turn[kind] % len(group)]
-            turn[kind] = turn[kind] + 1
+        table_at = 0
+        w1_codes_at = table_at + 2 * PACK * PASS
+        offer_at = table_at + 4 * T
+
+        banks = [psum.tile([P, HALF], F32, name="bank%d" % b) for b in range(8)]
+        rings = {"scalar": banks[:SCALAR_BANKS], "vector": banks[SCALAR_BANKS:]}
+        taken = {"scalar": 0, "vector": 0}
+
+        def next_bank(reader):
+            bank = rings[reader][taken[reader] % len(rings[reader])]
+            taken[reader] = taken[reader] + 1
             return bank
 
-        offsets = held("offsets", [P, S // 16], U16)
-        tab_w = [held("tab_w0", [P, T], U32), reuse.tile([P, T], U32, name="tab_w1", align_bytes=64, offset=0)]
+        offsets = held("offsets", [P, S // PER_COLUMN], U16)
+        tab_w = [held("tab_w0", [P, T], U32), placed("tab_w1", [P, T], U32, table_at)]
         tab_s = held("tab_s", [P, T], U8)
-        xs_w = [held("xs_w%d" % h, [P, HALF], U32) for h in range(2)]
+        xs_w = [held("xs_w%d" % half, [P, HALF], U32) for half in range(2)]
         xs_s = held("xs_s", [P, S], U8)
-        w2_raw_w = held("w2_raw_w", [P, 2 * H], U8)
-        w2_raw_s = held("w2_raw_s", [P, H], U8)
+        w2_given_w = held("w2_given_w", [P, 2 * H], U8)
+        w2_given_s = held("w2_given_s", [P, H], U8)
         w2_w = held("w2_w", [P, 2 * H], U8)
         w2_s = held("w2_s", [P, H], U8)
         w4_w = held("w4_w", [P, 2, N], U32)
         w5_w = held("w5_w", [P, 2, 2 * N], U8)
-        c1_t = held("c1_t", [P, 2, 4], F32)
-        c4_t = held("c4_t", [P, 3], F32)
-        w1_raw = {(a, g): held("w1_raw%d%d" % (a, g), [P, 4, PASS], F32) for a in range(2) for g in range(2)}
-        w3_raw = [held("w3_raw%d" % a, [P, 4, N], F32) for a in range(2)]
-        pol_t = [held("pol%d" % h, [P, 3, HALF], F32) for h in range(2)]
-        v_w = {}
-        v_all = {}
+        c1_t = held("c1_t", [P, 2, PACK], F32)
+        c4_t = held("c4_t", [P, N_TILES], F32)
+        w1_raw = {(a, g): held("w1_raw%d%d" % (a, g), [P, PACK, PASS], F32) for a in range(2) for g in range(2)}
+        w3_raw = [held("w3_raw%d" % g, [P, PACK, N], F32) for g in range(2)]
+        pol_t = [held("pol%d" % half, [P, N_TILES, HALF], F32) for half in range(2)]
         v_s = held("v_s", [P, S], U8)
-        v_s1 = held("v_s1", [P, S], U8)
-        w1_w = {}
-        w1_s = {(0, 0): w2_raw_s[4:P, 0:PASS], (1, 0): xs_s[4:P, 0:PASS],
-                (0, 1): xs_s[4:P, PASS:2 * PASS], (1, 1): w2_raw_s[4:P, PASS:2 * PASS]}
-        w3_w = {}
-        late_s = held("late_s", [P, S], U8)
+        v_s_moved = held("v_s_moved", [P, S], U8)
+        w3_w = held("w3_w", [P, 2 * N], U32)
         w3_s = held("w3_s", [P, 2 * N], U8)
-        w3_bs = {}
-        h_w = {(g, h): held("h_w%d%d" % (g, h), [P, HALF], U32) for g in range(2) for h in range(2)}
-        h_s = {(0, h): late_s[4:P, h * HALF:(h + 1) * HALF] for h in range(2)}
-        for h in range(2):
-            h_s[1, h] = held("h_s1%d" % h, [P, HALF], U8)[:]
-        warm_in = held("warm_in", [P, 8], F32)
-        warm_out = held("warm_out", [P, 8], F32)
+        h_w = {(g, half): held("h_w%d%d" % (g, half), [P, HALF], U32) for g in range(2) for half in range(2)}
+
+        w1_s = {(0, 0): w2_given_s[4:P, 0:PASS], (1, 0): xs_s[4:P, 0:PASS],
+                (0, 1): xs_s[4:P, PASS:2 * PASS], (1, 1): w2_given_s[4:P, PASS:2 * PASS]}
+        late_s = held("late_s", [P, S], U8)
+        h_s = {(0, half): late_s[4:P, half * HALF:(half + 1) * HALF] for half in range(2)}
+        for half in range(2):
+            h_s[1, half] = held("h_s1%d" % half, [P, HALF], U8)[:]
 
         nc.gpsimd.memset(tab_s[:].bitcast(I32), 0)
-        nc.vector.memset(warm_in[:], 0.0)
-        nc.vector.memset(v_s1[:].bitcast(I32), 0)
+        nc.vector.memset(v_s_moved[:].bitcast(I32), 0)
 
         def load_w1(a, g):
             rows = w1[a * PASS:(a + 1) * PASS, g * PASS:(g + 1) * PASS]
-            nc.sync.dma_start(out=w1_raw[a, g][:], in_=rows.rearrange("(p j) c -> p j c", j=4))
+            nc.sync.dma_start(out=w1_raw[a, g][:], in_=rows.rearrange("(p j) c -> p j c", j=PACK))
 
-        def load_tab(a):
+        def load_w3(g):
+            rows = w3[g * PASS:(g + 1) * PASS, :]
+            nc.sync.dma_start(out=w3_raw[g][:], in_=rows.rearrange("(p j) c -> p j c", j=PACK))
+
+        def load_table(a):
             nc.sync.dma_start(out=tab_w[a][:].bitcast(I32), in_=tab_words[a].rearrange("p t i -> p (t i)").bitcast(I32))
 
-        def load_xs(h):
+        def load_xs(half):
             words = xs_words[0].rearrange("p c i -> p (c i)").bitcast(I32)
-            nc.sync.dma_start(out=xs_w[h][:].bitcast(I32), in_=words[:, h * HALF:(h + 1) * HALF])
+            nc.sync.dma_start(out=xs_w[half][:].bitcast(I32), in_=words[:, half * HALF:(half + 1) * HALF])
 
-        def load_plane(queue, first, scales):
-            for q in range(4):
+        def load_one_pass_plane(plane, scales):
+            for q in range(QUADRANTS):
+                nc.sync.dma_start(out=plane[32 * q:32 * q + 4, :].bitcast(I32),
+                                  in_=scales[0, 4 * q:4 * q + 4, :].bitcast(I32))
+
+        def load_late_plane(first, scales):
+            for q in range(QUADRANTS):
                 rows = late_s[32 * q + first:32 * q + first + 4, 0:2 * N].rearrange("r (a c) -> r a c", a=2)
-                queue.dma_start(out=rows.bitcast(I32),
-                                in_=scales[:, 4 * q:4 * q + 4, :].rearrange("a r c -> r a c").bitcast(I32))
-
-        def load_plane1(queue, plane, scales):
-            for q in range(4):
-                queue.dma_start(out=plane[32 * q:32 * q + 4, :].bitcast(I32),
-                                in_=scales[0, 4 * q:4 * q + 4, :].bitcast(I32))
+                nc.sync.dma_start(out=rows.bitcast(I32),
+                                  in_=scales[:, 4 * q:4 * q + 4, :].rearrange("a r c -> r a c").bitcast(I32))
 
         nc.sync.dma_start(offsets[:], offs)
         load_w1(0, 0)
-        nc.sync.dma_start(out=w2_raw_w[:].bitcast(I32), in_=w2_words[0].bitcast(I32))
-        nc.sync.dma_start(out=c1_t[:], in_=c1.rearrange("(g p t) -> p g t", g=2, t=4))
-        for q in range(4):
+        nc.sync.dma_start(out=w2_given_w[:].bitcast(I32), in_=w2_words[0].bitcast(I32))
+        nc.gpsimd.dma_start(out=c1_t[:], in_=c1.rearrange("(g m t) -> m g t", g=2, t=PACK))
+        with nc.allow_non_contiguous_dma(reason="one bias value to a partition"):
+            nc.gpsimd.dma_start(out=c4_t[:], in_=c4.rearrange("(n p) -> p n", p=P))
+        for q in range(QUADRANTS):
             nc.scalar.dma_start(out=tab_s[32 * q:32 * q + 8, :].bitcast(I32),
                                 in_=tab_scales[:, 4 * q:4 * q + 4, :].bitcast(I32))
-        nc.scalar.activation(out=warm_out[:], in_=warm_in[:], func=ACT.Tanh)
-        load_tab(0)
+        load_table(0)
         load_w1(1, 0)
-        load_plane1(nc.sync, w2_raw_s, w2_scales)
-        load_tab(1)
-        load_plane1(nc.sync, xs_s, xs_scales)
+        load_one_pass_plane(w2_given_s, w2_scales)
         load_w1(0, 1)
+        load_one_pass_plane(xs_s, xs_scales)
+        load_table(1)
         load_xs(0)
-        load_plane(nc.sync, 0, w5_scales)
         load_w1(1, 1)
         load_xs(1)
-        load_plane(nc.sync, 8, w4_scales)
-        for a in range(2):
-            nc.sync.dma_start(out=w3_raw[a][:], in_=w3[a * PASS:(a + 1) * PASS, :].rearrange("(p j) c -> p j c", j=4))
+        load_late_plane(0, w5_scales)
+        load_w3(0)
+        load_late_plane(8, w4_scales)
+        load_w3(1)
         nc.sync.dma_start(out=w5_w[:].bitcast(I32), in_=w5_words.rearrange("a p c -> p a c").bitcast(I32))
         nc.sync.dma_start(out=w4_w[:].bitcast(I32), in_=w4_words.rearrange("a p c i -> p a (c i)").bitcast(I32))
-        with nc.allow_non_contiguous_dma(reason="one bias value to a partition"):
-            nc.sync.dma_start(out=c4_t[:], in_=c4.rearrange("(n p) -> p n", p=P))
-        for h in range(2):
-            nc.sync.dma_start(out=pol_t[h][:], in_=pol[:, h * HALF:(h + 1) * HALF].rearrange("(n p) j -> p n j", p=P))
+        for half in range(2):
+            columns = pol[:, half * HALF:(half + 1) * HALF]
+            nc.sync.dma_start(out=pol_t[half][:], in_=columns.rearrange("(n p) j -> p n j", p=P))
 
         def deal_w2_words():
-            nc.vector.tensor_copy(out=w2_w[:].bitcast(U16).rearrange("p (g t m) -> p g m t", g=2, t=4),
-                                  in_=w2_raw_w[:].bitcast(U16).rearrange("p (g m t) -> p g m t", g=2, t=4))
+            nc.vector.tensor_copy(out=w2_w[:].bitcast(U16).rearrange("p (g t m) -> p g m t", g=2, t=PACK),
+                                  in_=w2_given_w[:].bitcast(U16).rearrange("p (g m t) -> p g m t", g=2, t=PACK))
 
         def deal_w2_scales(g):
-            gc = slice(g * PASS, (g + 1) * PASS)
-            nc.vector.tensor_copy(out=w2_s[:, gc].rearrange("p (t m) -> p m t", t=4),
-                                  in_=w2_raw_s[:, gc].rearrange("p (m t) -> p m t", t=4))
+            group = slice(g * PASS, (g + 1) * PASS)
+            nc.vector.tensor_copy(out=w2_s[:, group].rearrange("p (t m) -> p m t", t=PACK),
+                                  in_=w2_given_s[:, group].rearrange("p (m t) -> p m t", t=PACK))
 
-        def listed(h):
-            return offsets[:, h * (HALF // 16):(h + 1) * (HALF // 16)]
+        def entries(half):
+            return slice(half * HALF, (half + 1) * HALF)
 
-        def gather_words(a, h):
-            if h == 0:
-                v_all[a] = held("v_w%d" % a, [P, S], U32, tag="w1_b10" if a == 1 else None)
-            v_w[a, h] = v_all[a][:, h * HALF:(h + 1) * HALF]
-            nc.vector.tensor_copy(out=v_w[a, h], in_=tab_w[a][:].indirect(listed(h)))
+        def listed(half):
+            return offsets[:, half * HALF // PER_COLUMN:(half + 1) * HALF // PER_COLUMN]
 
-        def gather_scales(h):
-            nc.vector.tensor_copy(out=v_s[:, h * HALF:(h + 1) * HALF], in_=tab_s[:].indirect(listed(h)))
+        v_w = {}
+
+        def gather_words(a):
+            v_w[a] = held("v_w%d" % a, [P, S], U32, tag="w1_b10" if a == 1 else None)
+            for half in range(2):
+                nc.vector.tensor_copy(out=v_w[a][:, entries(half)], in_=tab_w[a][:].indirect(listed(half)))
+
+        def gather_scales():
+            for half in range(2):
+                nc.vector.tensor_copy(out=v_s[:, entries(half)], in_=tab_s[:].indirect(listed(half)))
+            nc.gpsimd.dma_start(out=v_s_moved[0:LIVE_ROWS, :].bitcast(I32), in_=v_s[4:4 + LIVE_ROWS, :].bitcast(I32))
 
         w1_b = {}
+        w1_w = {}
 
-        def cast_w1(a, g):
-            if (a, g) == (0, 1):
-                tile = reuse.tile([P, 4 * PASS], BF16, name="w1_b01", align_bytes=64, offset=0)
-            else:
-                tile = held("w1_b%d%d" % (a, g), [P, 4 * PASS], BF16)
-            w1_b[a, g] = tile
-            order = "p m t j" if (a, g) == (1, 1) else "p m j t"
-            dst = tile[:].rearrange("p (t m j) -> " + order, t=4, j=4)
-            src = w1_raw[a, g][:].rearrange("p j (m t) -> " + order, t=4)
-            for m0 in range(0, P, 64):
-                if g == 0:
-                    nc.scalar.copy(out=dst[:, m0:m0 + 64], in_=src[:, m0:m0 + 64])
-                elif a == 1:
-                    nc.gpsimd.tensor_scalar(out=dst[:, m0:m0 + 64], in0=src[:, m0:m0 + 64], scalar1=1.0, scalar2=0.0,
-                                            op0=ALU.mult, op1=ALU.add)
-            if (a, g) == (0, 1):
-                nc.vector.tensor_copy(out=dst, in_=src)
+        def w1_views(a, g):
+            return (w1_b[a, g][:].rearrange("p (t m j) -> p m j t", t=PACK, j=PACK),
+                    w1_raw[a, g][:].rearrange("p j (m t) -> p m j t", t=PACK))
 
-        def quant_w1(a, g):
-            if (a, g) == (1, 1):
-                w1_w[a, g] = reuse.tile([P, PASS], U32, name="w1_w11", align_bytes=64, offset=8192)
+        def round_w1_on_scalar(a, g):
+            w1_b[a, g] = held("w1_b%d%d" % (a, g), [P, PACK * PASS], BF16)
+            dst, src = w1_views(a, g)
+            for m0 in range(0, P, P // 2):
+                nc.scalar.copy(out=dst[:, m0:m0 + P // 2], in_=src[:, m0:m0 + P // 2])
+
+        def round_last_w1_on_vector():
+            w1_b[1, 1] = placed("w1_b11", [P, PACK * PASS], BF16, table_at)
+            dst, src = w1_views(1, 1)
+            nc.vector.tensor_copy(out=dst, in_=src)
+
+        def quantise_w1(a, g):
+            if (a, g) == (0, 1):
+                w1_w[a, g] = placed("w1_w01", [P, PASS], U32, w1_codes_at)
             else:
                 w1_w[a, g] = held("w1_w%d%d" % (a, g), [P, PASS], U32)
             nc.vector.quantize_mx(out=w1_w[a, g][:].bitcast(FP8X4), scales=w1_s[a, g], in_=w1_b[a, g][:])
 
-        def cast_w3(a):
-            if a == 0:
-                w3_bs[a] = reuse.tile([P, N * 4], BF16, name="w3_b0", align_bytes=64, offset=8192 + 2048)
+        w3_b = {}
+
+        def round_w3(g):
+            if g == 0:
+                w3_b[g] = placed("w3_b0", [P, PACK * N], BF16, offer_at)
             else:
-                w3_bs[a] = held("w3_b1", [P, N * 4], BF16, tag="offer01")
-            dst = w3_bs[a][:].rearrange("p (c i j) -> p c j i", i=4, j=4)
-            src = w3_raw[a][:].rearrange("p j (c i) -> p c j i", i=4)
+                w3_b[g] = held("w3_b1", [P, PACK * N], BF16, tag="offer01")
+            dst = w3_b[g][:].rearrange("p (c i j) -> p c j i", i=4, j=PACK)
+            src = w3_raw[g][:].rearrange("p j (c i) -> p c j i", i=4)
             for c0 in range(0, N // 4, N // 8):
                 nc.scalar.copy(out=dst[:, c0:c0 + N // 8], in_=src[:, c0:c0 + N // 8])
 
-        def quant_w3(a):
-            if a == 0:
-                w3_w[0] = held("w3_w", [P, 2 * N], U32)
-            for c0, c1_ in ((0, 256), (256, 384)):
-                nc.vector.quantize_mx(out=w3_w[0][:, a * N + c0:a * N + c1_].bitcast(FP8X4),
-                                      scales=w3_s[:, a * N + c0:a * N + c1_], in_=w3_bs[a][:, 4 * c0:4 * c1_])
+        def quantise_w3(g):
+            for lo, hi in ((0, 2 * P), (2 * P, N)):
+                nc.vector.quantize_mx(out=w3_w[:, g * N + lo:g * N + hi].bitcast(FP8X4),
+                                      scales=w3_s[:, g * N + lo:g * N + hi], in_=w3_b[g][:, PACK * lo:PACK * hi])
 
-        h_bs = {}
+        h_b = {}
 
-        def quant_h(g, h):
-            nc.vector.quantize_mx(out=h_w[g, h][:].bitcast(FP8X4), scales=h_s[g, h], in_=h_bs[g, h][:])
+        def quantise_h(g, half):
+            nc.vector.quantize_mx(out=h_w[g, half][:].bitcast(FP8X4), scales=h_s[g, half], in_=h_b[g, half][:])
 
-        def meet(g, h, after_first=None):
-            cols = slice(h * HALF, (h + 1) * HALF)
-            if (g, h) == (0, 0):
-                offer = reuse.tile([P, 4, HALF], F32, name="offer00", align_bytes=64, offset=8192)
+        def meet(g, half, pending=None):
+            if (g, half) == (0, 0):
+                offer = placed("offer00", [P, PACK, HALF], F32, offer_at)
             else:
-                offer = held("offer%d%d" % (g, h), [P, 4, HALF], F32)
-            for t in range(4):
-                bank = next_bank("s")
-                wc = slice(t * P, (t + 1) * P)
+                offer = held("offer%d%d" % (g, half), [P, PACK, HALF], F32)
+            for t in range(PACK):
+                bank = next_bank("scalar")
+                dealt = slice(t * P, (t + 1) * P)
                 for a in range(2):
-                    nc.tensor.matmul_mx(out=bank[:], lhsT=w1_w[a, g][:, wc].bitcast(FP8X4), lhsT_scale=w1_s[a, g][:, wc],
-                                        rhs=v_w[a, h].bitcast(FP8X4), rhs_scale=v_s[4 * a:P, cols],
-                                        start=(a == 0), stop=(a == 1))
+                    nc.tensor.matmul_mx(out=bank[:], lhsT=w1_w[a, g][:, dealt].bitcast(FP8X4),
+                                        lhsT_scale=w1_s[a, g][:, dealt],
+                                        rhs=v_w[a][:, entries(half)].bitcast(FP8X4),
+                                        rhs_scale=v_s[4 * a:P, entries(half)], start=(a == 0), stop=(a == 1))
                 nc.scalar.activation(out=offer[:, t, :], in_=bank[:], func=ACT.Identity, bias=c1_t[:, g, t:t + 1])
-            h_b = held("h_b%d%d" % (g, h), [P, 4 * HALF], BF16)
-            h_bs[g, h] = h_b
-            for q in range(4):
-                bank = next_bank("v")
-                for t in range(4):
+            h_b[g, half] = held("h_b%d%d" % (g, half), [P, PACK * HALF], BF16)
+            for q in range(HALF // P):
+                bank = next_bank("vector")
+                within = slice(q * P, (q + 1) * P)
+                for t in range(PACK):
                     c0 = g * PASS + t * P
                     nc.tensor.matmul_mx(out=bank[:, t * P:(t + 1) * P],
                                         lhsT=w2_w[:, 2 * c0:2 * (c0 + P)].bitcast(FP4X4), lhsT_scale=w2_s[:, c0:c0 + P],
-                                        rhs=xs_w[h][:, q * P:(q + 1) * P].bitcast(FP8X4),
-                                        rhs_scale=xs_s[:, h * HALF + q * P:h * HALF + (q + 1) * P],
+                                        rhs=xs_w[half][:, within].bitcast(FP8X4),
+                                        rhs_scale=xs_s[:, half * HALF + q * P:half * HALF + (q + 1) * P],
                                         start=True, stop=True)
                 nc.vector.tensor_tensor(
-                    out=h_b[:, q * 4 * P:(q + 1) * 4 * P].rearrange("p (c i t) -> p c t i", i=4, t=4),
-                    in0=bank[:].rearrange("p (t c i) -> p c t i", t=4, i=4),
-                    in1=offer[:, :, q * P:(q + 1) * P].rearrange("p t (c i) -> p c t i", i=4),
+                    out=h_b[g, half][:, q * PACK * P:(q + 1) * PACK * P].rearrange("p (c i t) -> p c t i", i=4, t=PACK),
+                    in0=bank[:].rearrange("p (t c i) -> p c t i", t=PACK, i=4),
+                    in1=offer[:, :, within].rearrange("p t (c i) -> p c t i", i=4),
                     op=ALU.min)
-                if q == 0 and after_first is not None:
-                    after_first()
+                if q == 0 and pending is not None:
+                    quantise_h(*pending)
 
-        def read_out(h, after_first=None):
-            cols = slice(h * HALF, (h + 1) * HALF)
+        def read_out(half, pending=None):
             plain = {}
-            for n in range(3):
-                nc_ = slice(n * P, (n + 1) * P)
-                pre = next_bank("s")
+            for n in range(N_TILES):
+                bank = next_bank("scalar")
                 for g in range(2):
-                    nc.tensor.matmul_mx(out=pre[:], lhsT=w4_w[:, g, nc_].bitcast(FP8X4),
+                    nc.tensor.matmul_mx(out=bank[:], lhsT=w4_w[:, g, n * P:(n + 1) * P].bitcast(FP8X4),
                                         lhsT_scale=late_s[8:P, g * N + n * P:g * N + (n + 1) * P],
-                                        rhs=h_w[g, h][:].bitcast(FP8X4), rhs_scale=h_s[g, h],
+                                        rhs=h_w[g, half][:].bitcast(FP8X4), rhs_scale=h_s[g, half],
                                         start=(g == 0), stop=(g == 1))
-                plain[n] = ring3.tile([P, HALF], F32, name="plain")
-                nc.scalar.activation(out=plain[n][:], in_=pre[:], func=ACT.Tanh, bias=c4_t[:, n:n + 1])
-            for n in range(3):
-                nc_ = slice(n * P, (n + 1) * P)
-                own = next_bank("v")
+                plain[n] = stage.tile([P, HALF], F32, name="plain")
+                nc.scalar.activation(out=plain[n][:], in_=bank[:], func=ACT.Tanh, bias=c4_t[:, n:n + 1])
+            for n in range(N_TILES):
+                own = next_bank("vector")
                 for a in range(2):
-                    plane = v_s if a == 0 else v_s1
+                    plane = v_s if a == 0 else v_s_moved
                     nc.tensor.matmul_mx(out=own[:], lhsT=w5_w[:, a, 2 * n * P:2 * (n + 1) * P].bitcast(FP4X4),
                                         lhsT_scale=late_s[:, a * N + n * P:a * N + (n + 1) * P],
-                                        rhs=v_w[a, h].bitcast(FP8X4),
-                                        rhs_scale=plane[:, cols], start=(a == 0), stop=(a == 1))
-                part = ring3.tile([P, HALF], F32, name="part")
-                nc.vector.tensor_tensor(out=part[:], in0=own[:], in1=plain[n][:], op=ALU.add)
-                if n == 0 and after_first is not None:
-                    after_first()
-                last = (h, n) == (1, 2)
-                width = HALF // 2 if last else HALF
+                                        rhs=v_w[a][:, entries(half)].bitcast(FP8X4),
+                                        rhs_scale=plane[:, entries(half)], start=(a == 0), stop=(a == 1))
+                unruled = stage.tile([P, HALF], F32, name="unruled")
+                nc.vector.tensor_tensor(out=unruled[:], in0=own[:], in1=plain[n][:], op=ALU.add)
+                if n == 0 and pending is not None:
+                    quantise_h(*pending)
+                width = HALF // 2 if (half, n) == (1, N_TILES - 1) else HALF
                 for c0 in range(0, HALF, width):
-                    pc = slice(c0, c0 + width)
-                    raw = next_bank("v")
+                    piece = slice(c0, c0 + width)
+                    bank = next_bank("vector")
                     for g in range(2):
-                        wc = slice(g * N + n * P, g * N + (n + 1) * P)
-                        nc.tensor.matmul_mx(out=raw[:, 0:width], lhsT=w3_w[0][:, wc].bitcast(FP8X4),
-                                            lhsT_scale=w3_s[:, wc],
-                                            rhs=h_w[g, h][:, pc].bitcast(FP8X4), rhs_scale=h_s[g, h][:, pc],
+                        w3_columns = slice(g * N + n * P, g * N + (n + 1) * P)
+                        nc.tensor.matmul_mx(out=bank[:, 0:width], lhsT=w3_w[:, w3_columns].bitcast(FP8X4),
+                                            lhsT_scale=w3_s[:, w3_columns],
+                                            rhs=h_w[g, half][:, piece].bitcast(FP8X4), rhs_scale=h_s[g, half][:, piece],
                                             start=(g == 0), stop=(g == 1))
-                    ruled = ring3.tile([P, width], F32, name="ruled")
-                    nc.vector.tensor_tensor(out=ruled[:], in0=raw[:, 0:width], in1=pol_t[h][:, n, pc], op=ALU.mult)
-                    total = ring3.tile([P, width], F32, name="total")
-                    eng = nc.gpsimd if FINAL_ON_GPSIMD and not last else nc.vector
-                    eng.tensor_tensor(out=total[:], in0=ruled[:], in1=part[:, pc], op=ALU.add)
-                    nc.sync.dma_start(out=out[nc_, h * HALF + c0:h * HALF + c0 + width], in_=total[:])
+                    ruled = stage.tile([P, width], F32, name="ruled")
+                    nc.vector.tensor_tensor(out=ruled[:], in0=bank[:, 0:width], in1=pol_t[half][:, n, piece], op=ALU.mult)
+                    total = stage.tile([P, width], F32, name="total")
+                    adder = nc.gpsimd if half == 0 else nc.vector
+                    adder.tensor_tensor(out=total[:], in0=ruled[:], in1=unruled[:, piece], op=ALU.add)
+                    nc.sync.dma_start(out=out[n * P:(n + 1) * P, half * HALF + c0:half * HALF + c0 + width], in_=total[:])
 
         deal_w2_words()
-        gather_scales(0)
-        gather_scales(1)
-        nc.gpsimd.dma_start(out=v_s1[0:100, :].bitcast(I32), in_=v_s[4:104, :].bitcast(I32))
-        cast_w1(0, 0)
-        gather_words(0, 0)
-        gather_words(0, 1)
-        quant_w1(0, 0)
+        gather_scales()
+        round_w1_on_scalar(0, 0)
+        gather_words(0)
+        quantise_w1(0, 0)
         deal_w2_scales(0)
-        cast_w1(1, 0)
-        quant_w1(1, 0)
-        gather_words(1, 0)
-        gather_words(1, 1)
-        cast_w1(0, 1)
-        quant_w1(0, 1)
-        cast_w1(1, 1)
-        meet(0, 0)
-        quant_w1(1, 1)
+        round_w1_on_scalar(1, 0)
+        quantise_w1(1, 0)
+        round_w1_on_scalar(0, 1)
+        gather_words(1)
+        round_last_w1_on_vector()
+        quantise_w1(0, 1)
+        quantise_w1(1, 1)
         deal_w2_scales(1)
-        meet(0, 1, lambda: quant_h(0, 0))
-        cast_w3(0)
-        meet(1, 0, lambda: quant_h(0, 1))
-        cast_w3(1)
-        quant_w3(0)
-        quant_w3(1)
-        meet(1, 1, lambda: quant_h(1, 0))
-        read_out(0, lambda: quant_h(1, 1))
+        meet(0, 0)
+        meet(0, 1, pending=(0, 0))
+        round_w3(0)
+        meet(1, 0, pending=(0, 1))
+        round_w3(1)
+        quantise_w3(0)
+        quantise_w3(1)
+        meet(1, 1, pending=(1, 0))
+        read_out(0, pending=(1, 1))
         read_out(1)

from contextlib import ExitStack

import concourse.mybir as mybir

K, K2, H, N, T, S = 1024, 512, 1024, 384, 2048, 1024
FLOPS = 2 * S * (K * H + K2 * H + 2 * H * N + K * N)

F32 = mybir.dt.float32
BF16 = mybir.dt.bfloat16
I32 = mybir.dt.int32
U32 = mybir.dt.uint32
U16 = mybir.dt.uint16
U8 = mybir.dt.uint8
FP8X4 = mybir.dt.float8_e4m3fn_x4
FP4X4 = mybir.dt.float4_e2m1fn_x4
ALU = mybir.AluOpType
ACT = mybir.ActivationFunctionType

P = 128
PACK = 4
PASS = P * PACK
HALF = 512
QUADRANTS = 4
N_TILES = N // P
PER_COLUMN = 16
SCALAR_BANKS = 3
STAGE_BUFS = 2 * N_TILES
LIVE_ROWS = 100


def tile_list_housing_shortlist_features_kernel(
    tc, tab_words, tab_scales, offs, xs_words, xs_scales, w1, c1, w2_words, w2_scales,
    w3, pol, w4_words, w4_scales, c4, w5_words, w5_scales, out,
):
    nc = tc.nc
    with ExitStack() as ctx:
        keep = ctx.enter_context(tc.tile_pool(name="keep", bufs=1))
        stage = ctx.enter_context(tc.tile_pool(name="stage", bufs=STAGE_BUFS))
        reuse = ctx.enter_context(tc.tile_pool(name="reuse", bufs=1))
        psum = ctx.enter_context(tc.psum_pool(name="psum", bufs=1))

        def held(name, shape, dtype, tag=None):
            return keep.tile(shape, dtype, name=name, tag=tag or name, align_bytes=64)

        def placed(name, shape, dtype, offset):
            return reuse.tile(shape, dtype, name=name, align_bytes=64, offset=offset)

        table_at = 0
        w1_codes_at = table_at + 2 * PACK * PASS
        offer_at = table_at + 4 * T

        banks = [psum.tile([P, HALF], F32, name="bank%d" % b) for b in range(8)]
        rings = {"scalar": banks[:SCALAR_BANKS], "vector": banks[SCALAR_BANKS:]}
        taken = {"scalar": 0, "vector": 0}

        def next_bank(reader):
            bank = rings[reader][taken[reader] % len(rings[reader])]
            taken[reader] = taken[reader] + 1
            return bank

        offsets = held("offsets", [P, S // PER_COLUMN], U16)
        tab_w = [held("tab_w0", [P, T], U32), placed("tab_w1", [P, T], U32, table_at)]
        tab_s = held("tab_s", [P, T], U8)
        xs_w = [held("xs_w%d" % half, [P, HALF], U32) for half in range(2)]
        xs_s = held("xs_s", [P, S], U8)
        w2_given_w = held("w2_given_w", [P, 2 * H], U8)
        w2_given_s = held("w2_given_s", [P, H], U8)
        w2_w = held("w2_w", [P, 2 * H], U8)
        w2_s = held("w2_s", [P, H], U8)
        w4_w = held("w4_w", [P, 2, N], U32)
        w5_w = held("w5_w", [P, 2, 2 * N], U8)
        c1_t = held("c1_t", [P, 2, PACK], F32)
        c4_t = held("c4_t", [P, N_TILES], F32)
        w1_raw = {(a, g): held("w1_raw%d%d" % (a, g), [P, PACK, PASS], F32) for a in range(2) for g in range(2)}
        w3_raw = [held("w3_raw%d" % g, [P, PACK, N], F32) for g in range(2)]
        pol_t = [held("pol%d" % half, [P, N_TILES, HALF], F32) for half in range(2)]
        v_s = held("v_s", [P, S], U8)
        v_s_moved = held("v_s_moved", [P, S], U8)
        w3_w = held("w3_w", [P, 2 * N], U32)
        w3_s = held("w3_s", [P, 2 * N], U8)
        h_w = {(g, half): held("h_w%d%d" % (g, half), [P, HALF], U32) for g in range(2) for half in range(2)}

        w1_s = {(0, 0): w2_given_s[4:P, 0:PASS], (1, 0): xs_s[4:P, 0:PASS],
                (0, 1): xs_s[4:P, PASS:2 * PASS], (1, 1): w2_given_s[4:P, PASS:2 * PASS]}
        late_s = held("late_s", [P, S], U8)
        h_s = {(0, half): late_s[4:P, half * HALF:(half + 1) * HALF] for half in range(2)}
        for half in range(2):
            h_s[1, half] = held("h_s1%d" % half, [P, HALF], U8)[:]

        nc.gpsimd.memset(tab_s[:].bitcast(I32), 0)
        nc.vector.memset(v_s_moved[:].bitcast(I32), 0)

        def load_w1(a, g):
            rows = w1[a * PASS:(a + 1) * PASS, g * PASS:(g + 1) * PASS]
            nc.sync.dma_start(out=w1_raw[a, g][:], in_=rows.rearrange("(p j) c -> p j c", j=PACK))

        def load_w3(g):
            rows = w3[g * PASS:(g + 1) * PASS, :]
            nc.sync.dma_start(out=w3_raw[g][:], in_=rows.rearrange("(p j) c -> p j c", j=PACK))

        def load_table(a):
            nc.sync.dma_start(out=tab_w[a][:].bitcast(I32), in_=tab_words[a].rearrange("p t i -> p (t i)").bitcast(I32))

        def load_xs(half):
            words = xs_words[0].rearrange("p c i -> p (c i)").bitcast(I32)
            nc.sync.dma_start(out=xs_w[half][:].bitcast(I32), in_=words[:, half * HALF:(half + 1) * HALF])

        def load_one_pass_plane(plane, scales):
            for q in range(QUADRANTS):
                nc.sync.dma_start(out=plane[32 * q:32 * q + 4, :].bitcast(I32),
                                  in_=scales[0, 4 * q:4 * q + 4, :].bitcast(I32))

        def load_late_plane(first, scales):
            for q in range(QUADRANTS):
                rows = late_s[32 * q + first:32 * q + first + 4, 0:2 * N].rearrange("r (a c) -> r a c", a=2)
                nc.sync.dma_start(out=rows.bitcast(I32),
                                  in_=scales[:, 4 * q:4 * q + 4, :].rearrange("a r c -> r a c").bitcast(I32))

        nc.sync.dma_start(offsets[:], offs)
        load_w1(0, 0)
        nc.sync.dma_start(out=w2_given_w[:].bitcast(I32), in_=w2_words[0].bitcast(I32))
        nc.gpsimd.dma_start(out=c1_t[:], in_=c1.rearrange("(g m t) -> m g t", g=2, t=PACK))
        with nc.allow_non_contiguous_dma(reason="one bias value to a partition"):
            nc.gpsimd.dma_start(out=c4_t[:], in_=c4.rearrange("(n p) -> p n", p=P))
        for q in range(QUADRANTS):
            nc.scalar.dma_start(out=tab_s[32 * q:32 * q + 8, :].bitcast(I32),
                                in_=tab_scales[:, 4 * q:4 * q + 4, :].bitcast(I32))
        load_table(0)
        load_w1(1, 0)
        load_one_pass_plane(w2_given_s, w2_scales)
        load_w1(0, 1)
        load_one_pass_plane(xs_s, xs_scales)
        load_table(1)
        load_xs(0)
        load_w1(1, 1)
        load_xs(1)
        load_late_plane(0, w5_scales)
        load_w3(0)
        load_late_plane(8, w4_scales)
        load_w3(1)
        nc.sync.dma_start(out=w5_w[:].bitcast(I32), in_=w5_words.rearrange("a p c -> p a c").bitcast(I32))
        nc.sync.dma_start(out=w4_w[:].bitcast(I32), in_=w4_words.rearrange("a p c i -> p a (c i)").bitcast(I32))
        for half in range(2):
            columns = pol[:, half * HALF:(half + 1) * HALF]
            nc.sync.dma_start(out=pol_t[half][:], in_=columns.rearrange("(n p) j -> p n j", p=P))

        def deal_w2_words():
            nc.vector.tensor_copy(out=w2_w[:].bitcast(U16).rearrange("p (g t m) -> p g m t", g=2, t=PACK),
                                  in_=w2_given_w[:].bitcast(U16).rearrange("p (g m t) -> p g m t", g=2, t=PACK))

        def deal_w2_scales(g):
            group = slice(g * PASS, (g + 1) * PASS)
            nc.vector.tensor_copy(out=w2_s[:, group].rearrange("p (t m) -> p m t", t=PACK),
                                  in_=w2_given_s[:, group].rearrange("p (m t) -> p m t", t=PACK))

        def entries(half):
            return slice(half * HALF, (half + 1) * HALF)

        def listed(half):
            return offsets[:, half * HALF // PER_COLUMN:(half + 1) * HALF // PER_COLUMN]

        v_w = {}

        def gather_words(a):
            v_w[a] = held("v_w%d" % a, [P, S], U32, tag="w1_b10" if a == 1 else None)
            for half in range(2):
                nc.vector.tensor_copy(out=v_w[a][:, entries(half)], in_=tab_w[a][:].indirect(listed(half)))

        def gather_scales():
            for half in range(2):
                nc.vector.tensor_copy(out=v_s[:, entries(half)], in_=tab_s[:].indirect(listed(half)))
            nc.gpsimd.dma_start(out=v_s_moved[0:LIVE_ROWS, :].bitcast(I32), in_=v_s[4:4 + LIVE_ROWS, :].bitcast(I32))

        w1_b = {}
        w1_w = {}

        def w1_views(a, g):
            return (w1_b[a, g][:].rearrange("p (t m j) -> p m j t", t=PACK, j=PACK),
                    w1_raw[a, g][:].rearrange("p j (m t) -> p m j t", t=PACK))

        def round_w1_on_scalar(a, g):
            w1_b[a, g] = held("w1_b%d%d" % (a, g), [P, PACK * PASS], BF16)
            dst, src = w1_views(a, g)
            for m0 in range(0, P, P // 2):
                nc.scalar.copy(out=dst[:, m0:m0 + P // 2], in_=src[:, m0:m0 + P // 2])

        def round_last_w1_on_vector():
            w1_b[1, 1] = placed("w1_b11", [P, PACK * PASS], BF16, table_at)
            dst, src = w1_views(1, 1)
            nc.vector.tensor_copy(out=dst, in_=src)

        def quantise_w1(a, g):
            if (a, g) == (0, 1):
                w1_w[a, g] = placed("w1_w01", [P, PASS], U32, w1_codes_at)
            else:
                w1_w[a, g] = held("w1_w%d%d" % (a, g), [P, PASS], U32)
            nc.vector.quantize_mx(out=w1_w[a, g][:].bitcast(FP8X4), scales=w1_s[a, g], in_=w1_b[a, g][:])

        w3_b = {}

        def round_w3(g):
            if g == 0:
                w3_b[g] = placed("w3_b0", [P, PACK * N], BF16, offer_at)
            else:
                w3_b[g] = held("w3_b1", [P, PACK * N], BF16, tag="offer01")
            dst = w3_b[g][:].rearrange("p (c i j) -> p c j i", i=4, j=PACK)
            src = w3_raw[g][:].rearrange("p j (c i) -> p c j i", i=4)
            for c0 in range(0, N // 4, N // 8):
                nc.scalar.copy(out=dst[:, c0:c0 + N // 8], in_=src[:, c0:c0 + N // 8])

        def quantise_w3(g):
            for lo, hi in ((0, 2 * P), (2 * P, N)):
                nc.vector.quantize_mx(out=w3_w[:, g * N + lo:g * N + hi].bitcast(FP8X4),
                                      scales=w3_s[:, g * N + lo:g * N + hi], in_=w3_b[g][:, PACK * lo:PACK * hi])

        h_b = {}

        def quantise_h(g, half):
            nc.vector.quantize_mx(out=h_w[g, half][:].bitcast(FP8X4), scales=h_s[g, half], in_=h_b[g, half][:])

        def meet(g, half, pending=None):
            if (g, half) == (0, 0):
                offer = placed("offer00", [P, PACK, HALF], F32, offer_at)
            else:
                offer = held("offer%d%d" % (g, half), [P, PACK, HALF], F32)
            for t in range(PACK):
                bank = next_bank("scalar")
                dealt = slice(t * P, (t + 1) * P)
                for a in range(2):
                    nc.tensor.matmul_mx(out=bank[:], lhsT=w1_w[a, g][:, dealt].bitcast(FP8X4),
                                        lhsT_scale=w1_s[a, g][:, dealt],
                                        rhs=v_w[a][:, entries(half)].bitcast(FP8X4),
                                        rhs_scale=v_s[4 * a:P, entries(half)], start=(a == 0), stop=(a == 1))
                nc.scalar.activation(out=offer[:, t, :], in_=bank[:], func=ACT.Identity, bias=c1_t[:, g, t:t + 1])
            h_b[g, half] = held("h_b%d%d" % (g, half), [P, PACK * HALF], BF16)
            for q in range(HALF // P):
                bank = next_bank("vector")
                within = slice(q * P, (q + 1) * P)
                for t in range(PACK):
                    c0 = g * PASS + t * P
                    nc.tensor.matmul_mx(out=bank[:, t * P:(t + 1) * P],
                                        lhsT=w2_w[:, 2 * c0:2 * (c0 + P)].bitcast(FP4X4), lhsT_scale=w2_s[:, c0:c0 + P],
                                        rhs=xs_w[half][:, within].bitcast(FP8X4),
                                        rhs_scale=xs_s[:, half * HALF + q * P:half * HALF + (q + 1) * P],
                                        start=True, stop=True)
                nc.vector.tensor_tensor(
                    out=h_b[g, half][:, q * PACK * P:(q + 1) * PACK * P].rearrange("p (c i t) -> p c t i", i=4, t=PACK),
                    in0=bank[:].rearrange("p (t c i) -> p c t i", t=PACK, i=4),
                    in1=offer[:, :, within].rearrange("p t (c i) -> p c t i", i=4),
                    op=ALU.min)
                if q == 0 and pending is not None:
                    quantise_h(*pending)

        def read_out(half, pending=None):
            plain = {}
            for n in range(N_TILES):
                bank = next_bank("scalar")
                for g in range(2):
                    nc.tensor.matmul_mx(out=bank[:], lhsT=w4_w[:, g, n * P:(n + 1) * P].bitcast(FP8X4),
                                        lhsT_scale=late_s[8:P, g * N + n * P:g * N + (n + 1) * P],
                                        rhs=h_w[g, half][:].bitcast(FP8X4), rhs_scale=h_s[g, half],
                                        start=(g == 0), stop=(g == 1))
                plain[n] = stage.tile([P, HALF], F32, name="plain")
                nc.scalar.activation(out=plain[n][:], in_=bank[:], func=ACT.Tanh, bias=c4_t[:, n:n + 1])
            for n in range(N_TILES):
                own = next_bank("vector")
                for a in range(2):
                    plane = v_s if a == 0 else v_s_moved
                    nc.tensor.matmul_mx(out=own[:], lhsT=w5_w[:, a, 2 * n * P:2 * (n + 1) * P].bitcast(FP4X4),
                                        lhsT_scale=late_s[:, a * N + n * P:a * N + (n + 1) * P],
                                        rhs=v_w[a][:, entries(half)].bitcast(FP8X4),
                                        rhs_scale=plane[:, entries(half)], start=(a == 0), stop=(a == 1))
                unruled = stage.tile([P, HALF], F32, name="unruled")
                nc.vector.tensor_tensor(out=unruled[:], in0=own[:], in1=plain[n][:], op=ALU.add)
                if n == 0 and pending is not None:
                    quantise_h(*pending)
                width = HALF // 2 if (half, n) == (1, N_TILES - 1) else HALF
                for c0 in range(0, HALF, width):
                    piece = slice(c0, c0 + width)
                    bank = next_bank("vector")
                    for g in range(2):
                        w3_columns = slice(g * N + n * P, g * N + (n + 1) * P)
                        nc.tensor.matmul_mx(out=bank[:, 0:width], lhsT=w3_w[:, w3_columns].bitcast(FP8X4),
                                            lhsT_scale=w3_s[:, w3_columns],
                                            rhs=h_w[g, half][:, piece].bitcast(FP8X4), rhs_scale=h_s[g, half][:, piece],
                                            start=(g == 0), stop=(g == 1))
                    ruled = stage.tile([P, width], F32, name="ruled")
                    nc.vector.tensor_tensor(out=ruled[:], in0=bank[:, 0:width], in1=pol_t[half][:, n, piece], op=ALU.mult)
                    total = stage.tile([P, width], F32, name="total")
                    adder = nc.gpsimd if half == 0 else nc.vector
                    adder.tensor_tensor(out=total[:], in0=ruled[:], in1=unruled[:, piece], op=ALU.add)
                    nc.sync.dma_start(out=out[n * P:(n + 1) * P, half * HALF + c0:half * HALF + c0 + width], in_=total[:])

        deal_w2_words()
        gather_scales()
        round_w1_on_scalar(0, 0)
        gather_words(0)
        quantise_w1(0, 0)
        deal_w2_scales(0)
        round_w1_on_scalar(1, 0)
        quantise_w1(1, 0)
        round_w1_on_scalar(0, 1)
        gather_words(1)
        round_last_w1_on_vector()
        quantise_w1(0, 1)
        quantise_w1(1, 1)
        deal_w2_scales(1)
        meet(0, 0)
        meet(0, 1, pending=(0, 0))
        round_w3(0)
        meet(1, 0, pending=(0, 1))
        round_w3(1)
        quantise_w3(0)
        quantise_w3(1)
        meet(1, 1, pending=(1, 0))
        read_out(0, pending=(1, 1))
        read_out(1)
